import numpy as np
import ml_dtypes


def mxq(x, axis, fmt="e4m3"):
    dtype, down = {"e4m3": (ml_dtypes.float8_e4m3fn, 7), "e5m2": (ml_dtypes.float8_e5m2, 14)}[fmt]
    v = np.moveaxis(np.asarray(x, np.float32).astype(ml_dtypes.bfloat16).astype(np.float64), axis, -1)
    blocks = v.reshape(v.shape[:-1] + (-1, 32))
    amax = np.abs(blocks).max(-1, keepdims=True)
    byte = np.maximum(np.where(amax > 0, np.frexp(amax)[1] - 1 + 127, 0) - down, 1)
    scale = np.exp2(byte - 127.0)
    codes = (blocks / scale).astype(np.float32).astype(dtype).astype(np.float64)
    return np.moveaxis((codes * scale).reshape(v.shape), -1, axis)


WIDE = False


def mx_kscale(k):
    if not WIDE:
        return np.ones(k)
    levels = np.array([10, -10, 5, -5, 0])
    if k % 512:
        return np.exp2(np.random.permutation(np.resize(levels, k // 32))).repeat(32)
    a = np.empty((k // 512, 16))
    for p in range(k // 512):
        a[p, :8] = np.random.permutation(np.resize(levels, 8))
        for g in range(8):
            far = levels[np.abs(levels - a[p, g]) >= 10]
            a[p, g + 8] = far[np.random.randint(len(far))]
    return np.exp2(a.ravel()).repeat(32)


def f64(x):
    return np.asarray(x).astype(np.float64)


def striped(idx):
    return np.tile(idx.reshape(-1, 16).T, (8, 1)).astype(np.uint16)


def unstriped(offs):
    return offs[:16].T.reshape(-1).astype(np.int64)


E2M1 = np.array([0.0, 0.5, 1.0, 1.5, 2.0, 3.0, 4.0, 6.0, -0.0, -0.5, -1.0, -1.5, -2.0, -3.0, -4.0, -6.0])


def pack_weight(w, fmt):
    k, n = w.shape
    w = f64(np.asarray(w, np.float32).astype(ml_dtypes.bfloat16)).reshape(k // 32, 32, n)
    amax = np.abs(w).max(1)
    if fmt == "e4m3":
        byte = np.frexp(amax)[1] - 1 + 127 - 7
    else:
        mant, ex = np.frexp(amax / 6.0)
        byte = np.where(mant > 0.5, ex, ex - 1) + 127
    byte = np.clip(np.where(amax > 0, byte, 1), 1, 254)
    scaled = (w * np.exp2(127.0 - byte)[:, None, :]).reshape(k, n).astype(np.float32)
    by_word = np.ascontiguousarray(scaled.reshape(k // 512, 128, 4, n).transpose(0, 1, 3, 2))
    if fmt == "e4m3":
        words = by_word.astype(ml_dtypes.float8_e4m3fn).view(np.uint8)
    else:
        c = by_word.astype(ml_dtypes.float4_e2m1fn).view(np.uint8) & 0xF
        words = (c[..., 0::2] | (c[..., 1::2] << 4)).reshape(k // 512, 128, 2 * n)
    return np.ascontiguousarray(words), np.ascontiguousarray(byte.astype(np.uint8).reshape(k // 512, 16, n))


def unpack_weight(words, scales, fmt):
    g, _, n = scales.shape
    words = np.ascontiguousarray(words).reshape(g, 128, n, -1)
    if fmt == "e4m3":
        vals = words.view(ml_dtypes.float8_e4m3fn).astype(np.float64)
    else:
        nib = np.empty((g, 128, n, 4), np.uint8)
        nib[..., 0::2] = words & 0xF
        nib[..., 1::2] = words >> 4
        vals = E2M1[nib]
    vals = vals * np.repeat(np.exp2(scales.astype(np.float64) - 127.0), 8, axis=1)[..., None]
    return vals.transpose(0, 1, 3, 2).reshape(g * 512, n)


def gelu(v):
    return 0.5 * v * (1.0 + np.tanh(np.sqrt(2.0 / np.pi) * (v + 0.044715 * v**3)))


K, K2, T, TB, S, P, H, N = 1536, 1024, 4096, 2048, 1024, 512, 512, 384


def setup_inputs():
    n = np.random.standard_normal
    s, s2, u = mx_kscale(K)[:, None], mx_kscale(K2)[:, None], mx_kscale(H)[:, None]
    d = {}
    d["tab_words"], d["tab_scales"] = pack_weight(n((K, T)) * s, "e4m3")
    d["tab2_words"], d["tab2_scales"] = pack_weight(n((K2, TB)) * s2, "e4m3")
    d["w1"] = (0.54 * n((K, H)) / K**0.5 / s).astype(np.float32)
    d["gain"] = (np.exp(0.3 * n(H)) * u[:, 0]).astype(np.float32)
    d["w2"] = (0.8 * n((K2, H)) / K2**0.5 / s2 * u.T).astype(np.float32)
    d["w3_words"], d["w3_scales"] = pack_weight(n((K2, H)) / K2**0.5 / s2, "e2m1")
    d["wgs"] = np.exp(0.3 * n((128, P))).astype(np.float32)
    d["w4"] = (1.5 * n((H, N)) / H**0.5 / u).astype(np.float32)
    d["w5_words"], d["w5_scales"] = pack_weight(2.0 * n((H, N)) / H**0.5 / u, "e4m3")
    d["offs"] = striped(np.random.permutation(T)[:S])
    d["offs2"] = striped(np.random.permutation(TB)[:P])
    d["pos1"] = striped(np.random.permutation(S)[:P])
    return d


def reference(tab_words, tab_scales, tab2_words, tab2_scales, w1, gain, w2, w3_words, w3_scales,
              wgs, w4, w5_words, w5_scales, offs, offs2, pos1):
    v = unpack_weight(tab_words, tab_scales, "e4m3")[:, unstriped(offs)]
    v2 = unpack_weight(tab2_words, tab2_scales, "e4m3")[:, unstriped(offs2)]
    a = f64(gain)[:, None] * np.cos(mxq(f64(w1), 0, "e4m3").T @ v)
    m1 = mxq(f64(w2), 0, "e4m3").T @ v2
    m2 = unpack_weight(w3_words, w3_scales, "e2m1").T @ v2
    b = m1 * np.abs(m2)
    placed = np.zeros((H, S))
    placed[:, unstriped(pos1)] = np.tile(f64(wgs), (H // 128, 1)) * b
    z = a + placed
    y = mxq(f64(w4), 0, "e4m3").T @ mxq(z, 0, "e4m3")
    q = unpack_weight(w5_words, w5_scales, "e4m3").T @ mxq(a, 0, "e4m3")
    return y / (1.0 + np.abs(q))

@@ -1,0 +1,261 @@
+from contextlib import ExitStack
+
+import concourse.mybir as mybir
+
+K, K2, T, TB, S, M, H, N = 1536, 1024, 4096, 2048, 1024, 512, 512, 384
+FLOPS = 2 * (K * H * S + 2 * K2 * H * M + 2 * H * N * S)
+
+F32 = mybir.dt.float32
+BF16 = mybir.dt.bfloat16
+I32 = mybir.dt.int32
+U32 = mybir.dt.uint32
+U16 = mybir.dt.uint16
+U8 = mybir.dt.uint8
+FP8X4 = mybir.dt.float8_e4m3fn_x4
+FP4X4 = mybir.dt.float4_e2m1fn_x4
+ALU = mybir.AluOpType
+ACT = mybir.ActivationFunctionType
+
+P = 128
+PACK = 4
+QUADS = 4
+HALF = 512
+
+
+def tile_list_arousal_epoch_scorer_kernel(
+    tc, tab_words, tab_scales, tab2_words, tab2_scales, w1, gain, w2, w3_words, w3_scales,
+    wgs, w4, w5_words, w5_scales, offs, offs2, pos1, out,
+):
+    nc = tc.nc
+    passes1, passes2 = K // 512, K2 // 512
+
+    with ExitStack() as ctx:
+        keep = ctx.enter_context(tc.tile_pool(name="keep", bufs=1))
+        ring = ctx.enter_context(tc.tile_pool(name="ring", bufs=1))
+        psum = ctx.enter_context(tc.psum_pool(name="psum", bufs=1))
+
+        def held(shape, dtype, name):
+            return keep.tile(shape, dtype, name=name, align_bytes=64)
+
+        def wide_f32(shape, name):
+            return ring.tile(shape, F32, name=name, tag="wide_f32", bufs=4, align_bytes=64)
+
+        def row_f32(name):
+            return ring.tile([P, HALF], F32, name=name, tag="row_f32", bufs=8, align_bytes=64)
+
+        def wide_bf16(shape, name):
+            return ring.tile(shape, BF16, name=name, tag="wide_bf16", bufs=4, align_bytes=64)
+
+        banks = [psum.tile([P, HALF], F32, name="bank%d" % i) for i in range(8)]
+
+        def load_words(queue, tile, words):
+            queue.dma_start(out=tile.bitcast(I32), in_=words.bitcast(I32))
+
+        def load_planes_side_by_side(queue, tile, scales):
+            for q in range(QUADS):
+                load_words(queue, tile[32 * q : 32 * q + 4], scales[:, 4 * q : 4 * q + 4, :].rearrange("a r c -> r a c"))
+
+        offs_sb = keep.tile([P, S // 16], U16, name="offs_sb")
+        offs2_sb = keep.tile([P, M // 16], U16, name="offs2_sb")
+        pos_sb = keep.tile([P, M // 16], U16, name="pos_sb")
+
+        w3_raw_scales = held([P, passes2, H], U8, "w3_raw_scales")
+        tab2_planes = held([P, passes2, TB], U8, "tab2_planes")
+        tab_planes = held([P, T], U8, "tab_planes")
+        w5_planes = held([P, 1, N], U8, "w5_planes")
+        for tile in (w3_raw_scales, tab2_planes, tab_planes, w5_planes):
+            nc.vector.memset(tile[:].bitcast(I32), 0)
+        placed = [held([P, S], F32, "placed%d" % t) for t in range(PACK)]
+        for t in range(PACK):
+            nc.vector.memset(placed[t][:], 0.0)
+
+        tab2_sb = [held([P, TB], U32, "tab2_sb%d" % a) for a in range(passes2)]
+        tab_sb = [held([P, T], U32, "tab_sb%d" % a) for a in range(passes1)]
+        w3_raw = held([P, passes2, 2 * H], U8, "w3_raw")
+
+        def load_table(tile, words):
+            load_words(nc.sync, tile[:], words.rearrange("p t i -> p (t i)"))
+
+        def load_weight(w, a, name):
+            raw = wide_f32([P, PACK, w.shape[1]], name)
+            nc.sync.dma_start(out=raw[:], in_=w[512 * a : 512 * (a + 1), :].rearrange("(p j) c -> p j c", j=PACK))
+            return raw
+
+        def quantize(grouped, name):
+            width = grouped.shape[1] // PACK
+            codes = held([P, width], U32, name + "_codes")
+            plane = held([P, width], U8, name + "_plane")
+            nc.vector.quantize_mx(out=codes[:].bitcast(FP8X4), scales=plane[:], in_=grouped[:])
+            return codes, plane
+
+        def quantize_dealt(raw, name):
+            grouped = wide_bf16([P, PACK * H], name + "_bf16")
+            nc.scalar.copy(
+                out=grouped[:].rearrange("p (t m j) -> p m j t", t=PACK, j=PACK),
+                in_=raw[:].rearrange("p j (m t) -> p m j t", t=PACK),
+            )
+            return quantize(grouped, name)
+
+        def interleave(copy, rows, name):
+            width = rows.shape[2]
+            grouped = wide_bf16([P, PACK * width], name + "_bf16")
+            copy(
+                out=grouped[:].rearrange("p (c i t) -> p c t i", i=4, t=PACK),
+                in_=rows[:].rearrange("p t (c i) -> p c t i", i=4),
+            )
+            return quantize(grouped, name)
+
+        nc.sync.dma_start(offs2_sb[:], offs2)
+        load_table(tab2_sb[0], tab2_words[0])
+        load_planes_side_by_side(nc.sync, w3_raw_scales, w3_scales)
+        load_words(nc.sync, w3_raw[:], w3_words.rearrange("a p c -> p a c"))
+        w2_raw = [load_weight(w2, 0, "w2_raw0")]
+        load_planes_side_by_side(nc.sync, tab2_planes, tab2_scales)
+        w2_raw.append(load_weight(w2, 1, "w2_raw1"))
+        load_table(tab2_sb[1], tab2_words[1])
+        nc.sync.dma_start(offs_sb[:], offs)
+        wgs_sb = held([P, PACK, M], F32, "wgs_sb")
+        wgs_rows = wgs.rearrange("(p t) j -> p t j", t=PACK)
+        for q in range(QUADS):
+            nc.sync.dma_start(out=wgs_sb[32 * q : 32 * q + 32], in_=wgs_rows)
+        nc.sync.dma_start(pos_sb[:], pos1)
+        for q in range(QUADS):
+            load_words(nc.gpsimd, tab_planes[32 * q : 32 * q + 4 * passes1, :], tab_scales[:, 4 * q : 4 * q + 4, :])
+        gain_sb = held([P, PACK], F32, "gain_sb")
+        nc.gpsimd.dma_start(out=gain_sb[:], in_=gain.rearrange("(p t) -> p t", t=PACK))
+        load_planes_side_by_side(nc.gpsimd, w5_planes, w5_scales)
+
+        w3_sb = held([P, passes2, 2 * H], U8, "w3_sb")
+        w3_planes = held([P, passes2, H], U8, "w3_planes")
+        nc.scalar.copy(
+            out=w3_sb[:].bitcast(U16).rearrange("p a (t m) -> p a m t", t=PACK),
+            in_=w3_raw[:].bitcast(U16).rearrange("p a (m t) -> p a m t", t=PACK),
+        )
+        nc.vector.tensor_copy(
+            out=w3_planes[:].rearrange("p a (t m) -> p a m t", t=PACK),
+            in_=w3_raw_scales[:].rearrange("p a (m t) -> p a m t", t=PACK),
+        )
+
+        v2 = [held([P, M], U32, "v2_%d" % a) for a in range(passes2)]
+        v2_planes = [held([P, M], U8, "v2_plane%d" % a) for a in range(passes2)]
+        nc.vector.tensor_copy(v2[0][:], tab2_sb[0][:].indirect(offs2_sb[:]))
+        for a in range(passes2):
+            nc.vector.tensor_copy(v2_planes[a][:], tab2_planes[:, a, :].indirect(offs2_sb[:]))
+        w2_q = [quantize_dealt(w2_raw[a], "w2_%d" % a) for a in range(passes2)]
+        nc.vector.tensor_copy(v2[1][:], tab2_sb[1][:].indirect(offs2_sb[:]))
+        v_planes = held([P, S], U8, "v_planes")
+        nc.vector.tensor_copy(v_planes[:], tab_planes[:].indirect(offs_sb[:]))
+
+        w1_raw = []
+        for a in range(passes1):
+            w1_raw.append(load_weight(w1, a, "w1_raw%d" % a))
+            if a == passes1 - 1:
+                w4_raw = load_weight(w4, 0, "w4_raw")
+            load_table(tab_sb[a], tab_words[a])
+        w5_sb = held([P, N], U32, "w5_sb")
+        load_words(nc.sync, w5_sb[:], w5_words[0].rearrange("p c i -> p (c i)"))
+
+        def magnitude(t, m2):
+            for a in range(passes2):
+                nc.tensor.matmul_mx(
+                    out=m2[:], lhsT=w3_sb[:, a, 2 * P * t : 2 * P * (t + 1)].bitcast(FP4X4),
+                    lhsT_scale=w3_planes[:, a, P * t : P * (t + 1)], rhs=v2[a][:].bitcast(FP8X4),
+                    rhs_scale=v2_planes[a][:], start=(a == 0), stop=(a == passes2 - 1),
+                )
+            m2_abs = row_f32("m2_abs")
+            nc.scalar.activation(out=m2_abs[:], in_=m2[:], func=ACT.Abs)
+            return m2_abs
+
+        def marked(t, m1, m2_abs):
+            cols = slice(P * t, P * (t + 1))
+            for a in range(passes2):
+                nc.tensor.matmul_mx(
+                    out=m1[:], lhsT=w2_q[a][0][:, cols].bitcast(FP8X4), lhsT_scale=w2_q[a][1][:, cols],
+                    rhs=v2[a][:].bitcast(FP8X4), rhs_scale=v2_planes[a][:],
+                    start=(a == 0), stop=(a == passes2 - 1),
+                )
+            b_row = row_f32("b_row")
+            nc.vector.tensor_tensor(out=b_row[:], in0=m1[:], in1=m2_abs[:], op=ALU.mult)
+            return b_row
+
+        def scatter(t, b_row):
+            nc.vector.tensor_tensor(placed[t][:].indirect(pos_sb[:]), b_row[:], wgs_sb[:, t, :], ALU.mult)
+
+        m2_abs = [magnitude(t, banks[t]) for t in range(PACK)]
+        b_rows = [marked(t, banks[PACK + t], m2_abs[t]) for t in range(PACK - 1)]
+        for t in range(PACK - 1):
+            scatter(t, b_rows[t])
+
+        v = [held([P, S], U32, "v_%d" % a) for a in range(passes1)]
+        phase = [[banks[PACK * h + t] for t in range(PACK)] for h in range(2)]
+        for a in range(passes1):
+            w1_codes, w1_plane = quantize_dealt(w1_raw[a], "w1_%d" % a)
+            if a < passes1 - 1:
+                nc.vector.tensor_copy(v[a][:], tab_sb[a][:].indirect(offs_sb[:]))
+            else:
+                w4_codes, w4_plane = interleave(nc.scalar.copy, w4_raw, "w4")
+            for h in range(2):
+                epochs = slice(HALF * h, HALF * (h + 1))
+                if a == passes1 - 1:
+                    nc.vector.tensor_copy(v[a][:, epochs], tab_sb[a][:].indirect(offs_sb[:, 32 * h : 32 * (h + 1)]))
+                for t in range(PACK):
+                    cols = slice(P * t, P * (t + 1))
+                    nc.tensor.matmul_mx(
+                        out=phase[h][t][:], lhsT=w1_codes[:, cols].bitcast(FP8X4), lhsT_scale=w1_plane[:, cols],
+                        rhs=v[a][:, epochs].bitcast(FP8X4), rhs_scale=v_planes[4 * a :, epochs],
+                        start=(a == 0), stop=(a == passes1 - 1),
+                    )
+
+        gain_m2 = held([P, PACK], F32, "gain_m2")
+        nc.vector.tensor_scalar(out=gain_m2[:], in0=gain_sb[:], scalar1=-2.0, scalar2=None, op0=ALU.mult)
+
+        quantised = []
+        for h in range(2):
+            epochs = slice(HALF * h, HALF * (h + 1))
+            a_rows = wide_f32([P, PACK, HALF], "a_rows")
+            for t in range(PACK):
+                sine = row_f32("sine")
+                nc.scalar.activation(out=sine[:], in_=phase[h][t][:], func=ACT.Sin, scale=0.5)
+                if h == 0 and t == 0:
+                    scatter(PACK - 1, marked(PACK - 1, phase[h][t], m2_abs[PACK - 1]))
+                sine2 = row_f32("sine2")
+                nc.scalar.activation(out=sine2[:], in_=sine[:], func=ACT.Square)
+                nc.vector.tensor_scalar(
+                    out=a_rows[:, t, :], in0=sine2[:], scalar1=gain_m2[:, t : t + 1], scalar2=gain_sb[:, t : t + 1],
+                    op0=ALU.mult, op1=ALU.add,
+                )
+            a_q = interleave(nc.vector.tensor_copy, a_rows, "a_%d" % h)
+            z_rows = wide_bf16([P, PACK, HALF], "z_rows")
+            for t in range(PACK):
+                nc.vector.tensor_tensor(out=z_rows[:, t, :], in0=a_rows[:, t, :], in1=placed[t][:, epochs], op=ALU.add)
+            z_q = interleave(nc.vector.tensor_copy, z_rows, "z_%d" % h)
+            quantised.append((a_q, z_q))
+
+        for h in range(2):
+            epochs = slice(HALF * h, HALF * (h + 1))
+            (a_codes, a_plane), (z_codes, z_plane) = quantised[h]
+            damp = []
+            for n in range(N // P):
+                cols = slice(P * n, P * (n + 1))
+                q_sum = banks[(1 + n) if h == 0 else (7 + n) % 8]
+                nc.tensor.matmul_mx(
+                    out=q_sum[:], lhsT=w5_sb[:, cols].bitcast(FP8X4), lhsT_scale=w5_planes[:, 0, cols],
+                    rhs=a_codes[:].bitcast(FP8X4), rhs_scale=a_plane[:], start=True, stop=True,
+                )
+                q_abs = row_f32("q_abs")
+                nc.scalar.activation(out=q_abs[:], in_=q_sum[:], func=ACT.Abs)
+                root = row_f32("root")
+                nc.scalar.activation(out=root[:], in_=q_abs[:], func=ACT.Abs_reciprocal_sqrt, bias=1.0)
+                inverse = row_f32("inverse")
+                nc.scalar.activation(out=inverse[:], in_=root[:], func=ACT.Square)
+                damp.append(inverse)
+            for n in range(N // P):
+                cols = slice(P * n, P * (n + 1))
+                y_sum = banks[(4 + n) if h == 0 else 2 + n]
+                nc.tensor.matmul_mx(
+                    out=y_sum[:], lhsT=w4_codes[:, cols].bitcast(FP8X4), lhsT_scale=w4_plane[:, cols],
+                    rhs=z_codes[:].bitcast(FP8X4), rhs_scale=z_plane[:], start=True, stop=True,
+                )
+                score = row_f32("score")
+                nc.vector.tensor_tensor(out=score[:], in0=y_sum[:], in1=damp[n][:], op=ALU.mult)
+                nc.sync.dma_start(out=out[cols, epochs], in_=score[:])

@@ -38,10 +38,10 @@ def tile_list_arousal_epoch_scorer_kernel(
             return keep.tile(shape, dtype, name=name, align_bytes=64)
 
         def wide_f32(shape, name):
-            return ring.tile(shape, F32, name=name, tag="wide_f32", bufs=4, align_bytes=64)
+            return ring.tile(shape, F32, name=name, tag="wide_f32", bufs=5, align_bytes=64)
 
         def row_f32(name):
-            return ring.tile([P, HALF], F32, name=name, tag="row_f32", bufs=8, align_bytes=64)
+            return ring.tile([P, HALF], F32, name=name, tag="row_f32", bufs=6, align_bytes=64)
 
         def wide_bf16(shape, name):
             return ring.tile(shape, BF16, name=name, tag="wide_bf16", bufs=4, align_bytes=64)
@@ -51,9 +51,9 @@ def tile_list_arousal_epoch_scorer_kernel(
         def load_words(queue, tile, words):
             queue.dma_start(out=tile.bitcast(I32), in_=words.bitcast(I32))
 
-        def load_planes_side_by_side(queue, tile, scales):
-            for q in range(QUADS):
-                load_words(queue, tile[32 * q : 32 * q + 4], scales[:, 4 * q : 4 * q + 4, :].rearrange("a r c -> r a c"))
+        def load_planes_side_by_side(tile, scales, quadrants):
+            for q in quadrants:
+                load_words(nc.sync, tile[32 * q : 32 * q + 4], scales[:, 4 * q : 4 * q + 4, :].rearrange("a r c -> r a c"))
 
         offs_sb = keep.tile([P, S // 16], U16, name="offs_sb")
         offs2_sb = keep.tile([P, M // 16], U16, name="offs2_sb")
@@ -63,7 +63,9 @@ def tile_list_arousal_epoch_scorer_kernel(
         tab2_planes = held([P, passes2, TB], U8, "tab2_planes")
         tab_planes = held([P, T], U8, "tab_planes")
         w5_planes = held([P, 1, N], U8, "w5_planes")
-        for tile in (w3_raw_scales, tab2_planes, tab_planes, w5_planes):
+        nc.gpsimd.memset(tab2_planes[:, 0, :].bitcast(I32), 0)
+        nc.vector.memset(tab2_planes[:, 1, :].bitcast(I32), 0)
+        for tile in (w3_raw_scales, tab_planes, w5_planes):
             nc.vector.memset(tile[:].bitcast(I32), 0)
         placed = [held([P, S], F32, "placed%d" % t) for t in range(PACK)]
         for t in range(PACK):
@@ -81,59 +83,62 @@ def tile_list_arousal_epoch_scorer_kernel(
             nc.sync.dma_start(out=raw[:], in_=w[512 * a : 512 * (a + 1), :].rearrange("(p j) c -> p j c", j=PACK))
             return raw
 
-        def quantize(grouped, name):
+        def shared(shape, dtype, name, tag):
+            return ring.tile(shape, dtype, name=name, tag=tag, bufs=1, align_bytes=64)
+
+        def quantize(grouped, name, tag=None):
             width = grouped.shape[1] // PACK
-            codes = held([P, width], U32, name + "_codes")
+            codes = shared([P, width], U32, name + "_codes", tag or name)
             plane = held([P, width], U8, name + "_plane")
             nc.vector.quantize_mx(out=codes[:].bitcast(FP8X4), scales=plane[:], in_=grouped[:])
             return codes, plane
 
-        def quantize_dealt(raw, name):
-            grouped = wide_bf16([P, PACK * H], name + "_bf16")
-            nc.scalar.copy(
-                out=grouped[:].rearrange("p (t m j) -> p m j t", t=PACK, j=PACK),
-                in_=raw[:].rearrange("p j (m t) -> p m j t", t=PACK),
-            )
-            return quantize(grouped, name)
+        def quantize_dealt(raw, name, shares, bf16_tag=None, codes_tag=None):
+            if bf16_tag:
+                grouped = shared([P, PACK * H], BF16, name + "_bf16", bf16_tag)
+            else:
+                grouped = wide_bf16([P, PACK * H], name + "_bf16")
+            dealt = grouped[:].rearrange("p (t m j) -> p m t j", t=PACK, j=PACK)
+            given = raw[:].rearrange("p j (m t) -> p m t j", t=PACK)
+            for copy, rows in shares:
+                copy(out=dealt[:, rows], in_=given[:, rows])
+            return quantize(grouped, name, codes_tag)
 
         def interleave(copy, rows, name):
             width = rows.shape[2]
             grouped = wide_bf16([P, PACK * width], name + "_bf16")
             copy(
-                out=grouped[:].rearrange("p (c i t) -> p c t i", i=4, t=PACK),
-                in_=rows[:].rearrange("p t (c i) -> p c t i", i=4),
+                out=grouped[:].rearrange("p (c t) -> p c t", t=PACK),
+                in_=rows[:].rearrange("p t c -> p c t"),
             )
             return quantize(grouped, name)
 
+        for q in range(QUADS):
+            load_words(nc.gpsimd, tab_planes[32 * q : 32 * q + 4 * passes1, :], tab_scales[:, 4 * q : 4 * q + 4, :])
         nc.sync.dma_start(offs2_sb[:], offs2)
         load_table(tab2_sb[0], tab2_words[0])
-        load_planes_side_by_side(nc.sync, w3_raw_scales, w3_scales)
+        load_planes_side_by_side(tab2_planes, tab2_scales, range(QUADS))
         load_words(nc.sync, w3_raw[:], w3_words.rearrange("a p c -> p a c"))
-        w2_raw = [load_weight(w2, 0, "w2_raw0")]
-        load_planes_side_by_side(nc.sync, tab2_planes, tab2_scales)
-        w2_raw.append(load_weight(w2, 1, "w2_raw1"))
         load_table(tab2_sb[1], tab2_words[1])
+        load_planes_side_by_side(w3_raw_scales, w3_scales, range(QUADS))
+        w2_raw = [load_weight(w2, 0, "w2_raw0")]
         nc.sync.dma_start(offs_sb[:], offs)
+        nc.sync.dma_start(pos_sb[:], pos1)
+        w2_raw.append(load_weight(w2, 1, "w2_raw1"))
         wgs_sb = held([P, PACK, M], F32, "wgs_sb")
         wgs_rows = wgs.rearrange("(p t) j -> p t j", t=PACK)
         for q in range(QUADS):
             nc.sync.dma_start(out=wgs_sb[32 * q : 32 * q + 32], in_=wgs_rows)
-        nc.sync.dma_start(pos_sb[:], pos1)
-        for q in range(QUADS):
-            load_words(nc.gpsimd, tab_planes[32 * q : 32 * q + 4 * passes1, :], tab_scales[:, 4 * q : 4 * q + 4, :])
-        gain_sb = held([P, PACK], F32, "gain_sb")
-        nc.gpsimd.dma_start(out=gain_sb[:], in_=gain.rearrange("(p t) -> p t", t=PACK))
-        load_planes_side_by_side(nc.gpsimd, w5_planes, w5_scales)
 
         w3_sb = held([P, passes2, 2 * H], U8, "w3_sb")
         w3_planes = held([P, passes2, H], U8, "w3_planes")
         nc.scalar.copy(
-            out=w3_sb[:].bitcast(U16).rearrange("p a (t m) -> p a m t", t=PACK),
-            in_=w3_raw[:].bitcast(U16).rearrange("p a (m t) -> p a m t", t=PACK),
+            out=w3_sb[:].bitcast(U16).rearrange("p a (t m) -> p a t m", t=PACK),
+            in_=w3_raw[:].bitcast(U16).rearrange("p a (m t) -> p a t m", t=PACK),
         )
         nc.vector.tensor_copy(
-            out=w3_planes[:].rearrange("p a (t m) -> p a m t", t=PACK),
-            in_=w3_raw_scales[:].rearrange("p a (m t) -> p a m t", t=PACK),
+            out=w3_planes[:].rearrange("p a (t m) -> p a t m", t=PACK),
+            in_=w3_raw_scales[:].rearrange("p a (m t) -> p a t m", t=PACK),
         )
 
         v2 = [held([P, M], U32, "v2_%d" % a) for a in range(passes2)]
@@ -141,59 +146,70 @@ def tile_list_arousal_epoch_scorer_kernel(
         nc.vector.tensor_copy(v2[0][:], tab2_sb[0][:].indirect(offs2_sb[:]))
         for a in range(passes2):
             nc.vector.tensor_copy(v2_planes[a][:], tab2_planes[:, a, :].indirect(offs2_sb[:]))
-        w2_q = [quantize_dealt(w2_raw[a], "w2_%d" % a) for a in range(passes2)]
         nc.vector.tensor_copy(v2[1][:], tab2_sb[1][:].indirect(offs2_sb[:]))
+        scalar_alone = [(nc.scalar.copy, slice(0, P))]
+        both = [(nc.scalar.copy, slice(0, P // 2)), (nc.vector.tensor_copy, slice(P // 2, P))]
+        w2_q = [quantize_dealt(w2_raw[0], "w2_0", scalar_alone), quantize_dealt(w2_raw[1], "w2_1", both)]
         v_planes = held([P, S], U8, "v_planes")
         nc.vector.tensor_copy(v_planes[:], tab_planes[:].indirect(offs_sb[:]))
 
         w1_raw = []
         for a in range(passes1):
             w1_raw.append(load_weight(w1, a, "w1_raw%d" % a))
-            if a == passes1 - 1:
-                w4_raw = load_weight(w4, 0, "w4_raw")
             load_table(tab_sb[a], tab_words[a])
+        w4_raw = load_weight(w4, 0, "w4_raw")
+        gain_sb = held([P, PACK], F32, "gain_sb")
+        nc.sync.dma_start(out=gain_sb[:], in_=gain.rearrange("(p t) -> p t", t=PACK))
         w5_sb = held([P, N], U32, "w5_sb")
         load_words(nc.sync, w5_sb[:], w5_words[0].rearrange("p c i -> p (c i)"))
+        load_planes_side_by_side(w5_planes, w5_scales, range(QUADS))
+
+        def magnitude_pass(a, t, m2):
+            nc.tensor.matmul_mx(
+                out=m2[:], lhsT=w3_sb[:, a, 2 * P * t : 2 * P * (t + 1)].bitcast(FP4X4),
+                lhsT_scale=w3_planes[:, a, P * t : P * (t + 1)], rhs=v2[a][:].bitcast(FP8X4),
+                rhs_scale=v2_planes[a][:], start=(a == 0), stop=(a == passes2 - 1),
+            )
+
+        def signed_pass(a, t, m1):
+            cols = slice(P * t, P * (t + 1))
+            nc.tensor.matmul_mx(
+                out=m1[:], lhsT=w2_q[a][0][:, cols].bitcast(FP8X4), lhsT_scale=w2_q[a][1][:, cols],
+                rhs=v2[a][:].bitcast(FP8X4), rhs_scale=v2_planes[a][:],
+                start=(a == 0), stop=(a == passes2 - 1),
+            )
 
         def magnitude(t, m2):
-            for a in range(passes2):
-                nc.tensor.matmul_mx(
-                    out=m2[:], lhsT=w3_sb[:, a, 2 * P * t : 2 * P * (t + 1)].bitcast(FP4X4),
-                    lhsT_scale=w3_planes[:, a, P * t : P * (t + 1)], rhs=v2[a][:].bitcast(FP8X4),
-                    rhs_scale=v2_planes[a][:], start=(a == 0), stop=(a == passes2 - 1),
-                )
-            m2_abs = row_f32("m2_abs")
+            m2_abs = shared([P, M], F32, "m2_abs%d" % t, "after_b%d" % t)
             nc.scalar.activation(out=m2_abs[:], in_=m2[:], func=ACT.Abs)
             return m2_abs
 
         def marked(t, m1, m2_abs):
-            cols = slice(P * t, P * (t + 1))
-            for a in range(passes2):
-                nc.tensor.matmul_mx(
-                    out=m1[:], lhsT=w2_q[a][0][:, cols].bitcast(FP8X4), lhsT_scale=w2_q[a][1][:, cols],
-                    rhs=v2[a][:].bitcast(FP8X4), rhs_scale=v2_planes[a][:],
-                    start=(a == 0), stop=(a == passes2 - 1),
-                )
-            b_row = row_f32("b_row")
+            b_row = shared([P, M], F32, "b_row%d" % t, "after_scatter%d" % t)
             nc.vector.tensor_tensor(out=b_row[:], in0=m1[:], in1=m2_abs[:], op=ALU.mult)
             return b_row
 
         def scatter(t, b_row):
             nc.vector.tensor_tensor(placed[t][:].indirect(pos_sb[:]), b_row[:], wgs_sb[:, t, :], ALU.mult)
 
-        m2_abs = [magnitude(t, banks[t]) for t in range(PACK)]
-        b_rows = [marked(t, banks[PACK + t], m2_abs[t]) for t in range(PACK - 1)]
-        for t in range(PACK - 1):
+        last = PACK - 1
+        for t in range(PACK):
+            for a in range(passes2):
+                magnitude_pass(a, t, banks[t])
+                if t < last:
+                    signed_pass(a, t, banks[PACK + t])
+        magnitudes = [magnitude(t, banks[t]) for t in range(PACK)]
+        b_rows = [marked(t, banks[PACK + t], magnitudes[t]) for t in range(last)]
+        for t in range(last):
             scatter(t, b_rows[t])
 
-        v = [held([P, S], U32, "v_%d" % a) for a in range(passes1)]
+        v = [shared([P, S], U32, "v_%d" % a, "after_scatter%d" % min(a + 1, 2) if a < 2 else "v_last") for a in range(passes1)]
         phase = [[banks[PACK * h + t] for t in range(PACK)] for h in range(2)]
         for a in range(passes1):
-            w1_codes, w1_plane = quantize_dealt(w1_raw[a], "w1_%d" % a)
+            w1_codes, w1_plane = quantize_dealt(w1_raw[a], "w1_%d" % a, scalar_alone,
+                                                "after_b0" if a == 0 else None, "after_b%d" % (a + 1) if a < 2 else None)
             if a < passes1 - 1:
                 nc.vector.tensor_copy(v[a][:], tab_sb[a][:].indirect(offs_sb[:]))
-            else:
-                w4_codes, w4_plane = interleave(nc.scalar.copy, w4_raw, "w4")
             for h in range(2):
                 epochs = slice(HALF * h, HALF * (h + 1))
                 if a == passes1 - 1:
@@ -217,7 +233,9 @@ def tile_list_arousal_epoch_scorer_kernel(
                 sine = row_f32("sine")
                 nc.scalar.activation(out=sine[:], in_=phase[h][t][:], func=ACT.Sin, scale=0.5)
                 if h == 0 and t == 0:
-                    scatter(PACK - 1, marked(PACK - 1, phase[h][t], m2_abs[PACK - 1]))
+                    for a in range(passes2):
+                        signed_pass(a, last, phase[h][t])
+                    scatter(last, marked(last, phase[h][t], magnitudes[last]))
                 sine2 = row_f32("sine2")
                 nc.scalar.activation(out=sine2[:], in_=sine[:], func=ACT.Square)
                 nc.vector.tensor_scalar(
@@ -225,6 +243,8 @@ def tile_list_arousal_epoch_scorer_kernel(
                     op0=ALU.mult, op1=ALU.add,
                 )
             a_q = interleave(nc.vector.tensor_copy, a_rows, "a_%d" % h)
+            if h == 0:
+                w4_codes, w4_plane = interleave(nc.vector.tensor_copy, w4_raw, "w4")
             z_rows = wide_bf16([P, PACK, HALF], "z_rows")
             for t in range(PACK):
                 nc.vector.tensor_tensor(out=z_rows[:, t, :], in0=a_rows[:, t, :], in1=placed[t][:, epochs], op=ALU.add)

@@ -38,15 +38,18 @@ def tile_list_arousal_epoch_scorer_kernel(
             return keep.tile(shape, dtype, name=name, align_bytes=64)
 
         def wide_f32(shape, name):
-            return ring.tile(shape, F32, name=name, tag="wide_f32", bufs=5, align_bytes=64)
+            return ring.tile(shape, F32, name=name, tag="wide_f32", bufs=3, align_bytes=64)
 
         def row_f32(name):
-            return ring.tile([P, HALF], F32, name=name, tag="row_f32", bufs=6, align_bytes=64)
+            return ring.tile([P, HALF], F32, name=name, tag="row_f32", bufs=8, align_bytes=64)
 
         def wide_bf16(shape, name):
             return ring.tile(shape, BF16, name=name, tag="wide_bf16", bufs=4, align_bytes=64)
 
         banks = [psum.tile([P, HALF], F32, name="bank%d" % i) for i in range(8)]
+
+        def shared(shape, dtype, name, tag):
+            return ring.tile(shape, dtype, name=name, tag=tag, bufs=1, align_bytes=64)
 
         def load_words(queue, tile, words):
             queue.dma_start(out=tile.bitcast(I32), in_=words.bitcast(I32))
@@ -59,41 +62,40 @@ def tile_list_arousal_epoch_scorer_kernel(
         offs2_sb = keep.tile([P, M // 16], U16, name="offs2_sb")
         pos_sb = keep.tile([P, M // 16], U16, name="pos_sb")
 
-        w3_raw_scales = held([P, passes2, H], U8, "w3_raw_scales")
-        tab2_planes = held([P, passes2, TB], U8, "tab2_planes")
-        tab_planes = held([P, T], U8, "tab_planes")
+        w3_raw_scales = shared([P, passes2, H], U8, "w3_raw_scales", "w3_raw_scales")
+        tab2_planes = shared([P, passes2, TB], U8, "tab2_planes", "tab2_planes")
+        tab_planes = shared([P, T], U8, "tab_planes", "dealt_a")
         w5_planes = held([P, 1, N], U8, "w5_planes")
+        nc.gpsimd.memset(w3_raw_scales[:].bitcast(I32), 0)
         nc.gpsimd.memset(tab2_planes[:, 0, :].bitcast(I32), 0)
         nc.vector.memset(tab2_planes[:, 1, :].bitcast(I32), 0)
-        for tile in (w3_raw_scales, tab_planes, w5_planes):
+        for tile in (tab_planes, w5_planes):
             nc.vector.memset(tile[:].bitcast(I32), 0)
         placed = [held([P, S], F32, "placed%d" % t) for t in range(PACK)]
         for t in range(PACK):
             nc.vector.memset(placed[t][:], 0.0)
 
-        tab2_sb = [held([P, TB], U32, "tab2_sb%d" % a) for a in range(passes2)]
-        tab_sb = [held([P, T], U32, "tab_sb%d" % a) for a in range(passes1)]
+        tab2_sb = [shared([P, TB], U32, "tab2_sb%d" % a, "tab2_sb%d" % a) for a in range(passes2)]
+        tab_sb = [ring.tile([P, T], U32, name="tab_sb%d" % a, tag="tab_sb%d" % a, bufs=1, align_bytes=64) for a in range(passes1)]
         w3_raw = held([P, passes2, 2 * H], U8, "w3_raw")
 
         def load_table(tile, words):
             load_words(nc.sync, tile[:], words.rearrange("p t i -> p (t i)"))
 
-        def load_weight(w, a, name):
-            raw = wide_f32([P, PACK, w.shape[1]], name)
+        def load_weight(w, a, name, tag=None):
+            shape = [P, PACK, w.shape[1]]
+            raw = shared(shape, F32, name, tag) if tag else wide_f32(shape, name)
             nc.sync.dma_start(out=raw[:], in_=w[512 * a : 512 * (a + 1), :].rearrange("(p j) c -> p j c", j=PACK))
             return raw
 
-        def shared(shape, dtype, name, tag):
-            return ring.tile(shape, dtype, name=name, tag=tag, bufs=1, align_bytes=64)
-
-        def quantize(grouped, name, tag=None):
+        def quantize(grouped, name, tag=None, plane_tag=None):
             width = grouped.shape[1] // PACK
             codes = shared([P, width], U32, name + "_codes", tag or name)
-            plane = held([P, width], U8, name + "_plane")
+            plane = shared([P, width], U8, name + "_plane", plane_tag or name + "_plane")
             nc.vector.quantize_mx(out=codes[:].bitcast(FP8X4), scales=plane[:], in_=grouped[:])
             return codes, plane
 
-        def quantize_dealt(raw, name, shares, bf16_tag=None, codes_tag=None):
+        def quantize_dealt(raw, name, shares, bf16_tag=None, codes_tag=None, plane_tag=None):
             if bf16_tag:
                 grouped = shared([P, PACK * H], BF16, name + "_bf16", bf16_tag)
             else:
@@ -102,11 +104,14 @@ def tile_list_arousal_epoch_scorer_kernel(
             given = raw[:].rearrange("p j (m t) -> p m t j", t=PACK)
             for copy, rows in shares:
                 copy(out=dealt[:, rows], in_=given[:, rows])
-            return quantize(grouped, name, codes_tag)
+            return quantize(grouped, name, codes_tag, plane_tag)
 
-        def interleave(copy, rows, name):
+        def interleave(copy, rows, name, bf16_tag=None):
             width = rows.shape[2]
-            grouped = wide_bf16([P, PACK * width], name + "_bf16")
+            if bf16_tag:
+                grouped = shared([P, PACK * width], BF16, name + "_bf16", bf16_tag)
+            else:
+                grouped = wide_bf16([P, PACK * width], name + "_bf16")
             copy(
                 out=grouped[:].rearrange("p (c t) -> p c t", t=PACK),
                 in_=rows[:].rearrange("p t c -> p c t"),
@@ -116,50 +121,53 @@ def tile_list_arousal_epoch_scorer_kernel(
         for q in range(QUADS):
             load_words(nc.gpsimd, tab_planes[32 * q : 32 * q + 4 * passes1, :], tab_scales[:, 4 * q : 4 * q + 4, :])
         nc.sync.dma_start(offs2_sb[:], offs2)
-        load_table(tab2_sb[0], tab2_words[0])
-        load_planes_side_by_side(tab2_planes, tab2_scales, range(QUADS))
-        load_words(nc.sync, w3_raw[:], w3_words.rearrange("a p c -> p a c"))
-        load_table(tab2_sb[1], tab2_words[1])
-        load_planes_side_by_side(w3_raw_scales, w3_scales, range(QUADS))
-        w2_raw = [load_weight(w2, 0, "w2_raw0")]
         nc.sync.dma_start(offs_sb[:], offs)
         nc.sync.dma_start(pos_sb[:], pos1)
-        w2_raw.append(load_weight(w2, 1, "w2_raw1"))
+        gain_sb = held([P, PACK], F32, "gain_sb")
+        nc.sync.dma_start(out=gain_sb[:], in_=gain.rearrange("(p t) -> p t", t=PACK))
+        load_table(tab2_sb[0], tab2_words[0])
+        load_words(nc.sync, w3_raw[:], w3_words.rearrange("a p c -> p a c"))
+        load_planes_side_by_side(w3_raw_scales, w3_scales, range(QUADS))
         wgs_sb = held([P, PACK, M], F32, "wgs_sb")
         wgs_rows = wgs.rearrange("(p t) j -> p t j", t=PACK)
-        for q in range(QUADS):
+        nc.sync.dma_start(out=wgs_sb[0:32], in_=wgs_rows)
+        load_planes_side_by_side(tab2_planes, tab2_scales, range(QUADS))
+        load_table(tab2_sb[1], tab2_words[1])
+        w2_raw = [load_weight(w2, 0, "w2_raw0"), load_weight(w2, 1, "w2_raw1", "w2_last")]
+        for q in range(1, QUADS):
             nc.sync.dma_start(out=wgs_sb[32 * q : 32 * q + 32], in_=wgs_rows)
 
         w3_sb = held([P, passes2, 2 * H], U8, "w3_sb")
-        w3_planes = held([P, passes2, H], U8, "w3_planes")
+        w3_planes = shared([P, passes2, H], U8, "w3_planes", "tab2_sb0")
         nc.scalar.copy(
             out=w3_sb[:].bitcast(U16).rearrange("p a (t m) -> p a t m", t=PACK),
             in_=w3_raw[:].bitcast(U16).rearrange("p a (m t) -> p a t m", t=PACK),
         )
+
+        v2 = [held([P, M], U32, "v2_0"), shared([P, M], U32, "v2_1", "tab2_planes")]
+        v2_planes = [held([P, M], U8, "v2_plane%d" % a) for a in range(passes2)]
+        nc.vector.tensor_copy(v2[0][:], tab2_sb[0][:].indirect(offs2_sb[:]))
         nc.vector.tensor_copy(
             out=w3_planes[:].rearrange("p a (t m) -> p a t m", t=PACK),
             in_=w3_raw_scales[:].rearrange("p a (m t) -> p a t m", t=PACK),
         )
-
-        v2 = [held([P, M], U32, "v2_%d" % a) for a in range(passes2)]
-        v2_planes = [held([P, M], U8, "v2_plane%d" % a) for a in range(passes2)]
-        nc.vector.tensor_copy(v2[0][:], tab2_sb[0][:].indirect(offs2_sb[:]))
         for a in range(passes2):
             nc.vector.tensor_copy(v2_planes[a][:], tab2_planes[:, a, :].indirect(offs2_sb[:]))
         nc.vector.tensor_copy(v2[1][:], tab2_sb[1][:].indirect(offs2_sb[:]))
+        v_planes = shared([P, S], U8, "v_planes", "tab2_sb1")
+        nc.vector.tensor_copy(v_planes[:], tab_planes[:].indirect(offs_sb[:]))
         scalar_alone = [(nc.scalar.copy, slice(0, P))]
         both = [(nc.scalar.copy, slice(0, P // 2)), (nc.vector.tensor_copy, slice(P // 2, P))]
-        w2_q = [quantize_dealt(w2_raw[0], "w2_0", scalar_alone), quantize_dealt(w2_raw[1], "w2_1", both)]
-        v_planes = held([P, S], U8, "v_planes")
-        nc.vector.tensor_copy(v_planes[:], tab_planes[:].indirect(offs_sb[:]))
+        w2_q = [
+            quantize_dealt(w2_raw[0], "w2_0", scalar_alone, "dealt_b", None, "w3_raw_scales"),
+            quantize_dealt(w2_raw[1], "w2_1", both, "dealt_a"),
+        ]
 
         w1_raw = []
         for a in range(passes1):
             w1_raw.append(load_weight(w1, a, "w1_raw%d" % a))
             load_table(tab_sb[a], tab_words[a])
         w4_raw = load_weight(w4, 0, "w4_raw")
-        gain_sb = held([P, PACK], F32, "gain_sb")
-        nc.sync.dma_start(out=gain_sb[:], in_=gain.rearrange("(p t) -> p t", t=PACK))
         w5_sb = held([P, N], U32, "w5_sb")
         load_words(nc.sync, w5_sb[:], w5_words[0].rearrange("p c i -> p (c i)"))
         load_planes_side_by_side(w5_planes, w5_scales, range(QUADS))
@@ -179,14 +187,11 @@ def tile_list_arousal_epoch_scorer_kernel(
                 start=(a == 0), stop=(a == passes2 - 1),
             )
 
-        def magnitude(t, m2):
-            m2_abs = shared([P, M], F32, "m2_abs%d" % t, "after_b%d" % t)
-            nc.scalar.activation(out=m2_abs[:], in_=m2[:], func=ACT.Abs)
-            return m2_abs
+        magnitudes = shared([P, PACK, M], F32, "magnitudes", "w2_last")
 
-        def marked(t, m1, m2_abs):
+        def marked(t, m1):
             b_row = shared([P, M], F32, "b_row%d" % t, "after_scatter%d" % t)
-            nc.vector.tensor_tensor(out=b_row[:], in0=m1[:], in1=m2_abs[:], op=ALU.mult)
+            nc.vector.tensor_tensor(out=b_row[:], in0=m1[:], in1=magnitudes[:, t, :], op=ALU.mult)
             return b_row
 
         def scatter(t, b_row):
@@ -195,19 +200,18 @@ def tile_list_arousal_epoch_scorer_kernel(
         last = PACK - 1
         for t in range(PACK):
             for a in range(passes2):
-                magnitude_pass(a, t, banks[t])
+                magnitude_pass(a, t, banks[t % 2])
                 if t < last:
                     signed_pass(a, t, banks[PACK + t])
-        magnitudes = [magnitude(t, banks[t]) for t in range(PACK)]
-        b_rows = [marked(t, banks[PACK + t], magnitudes[t]) for t in range(last)]
-        for t in range(last):
-            scatter(t, b_rows[t])
+            nc.scalar.activation(out=magnitudes[:, t, :], in_=banks[t % 2][:], func=ACT.Abs)
+            if t < last:
+                scatter(t, marked(t, banks[PACK + t]))
 
         v = [shared([P, S], U32, "v_%d" % a, "after_scatter%d" % min(a + 1, 2) if a < 2 else "v_last") for a in range(passes1)]
         phase = [[banks[PACK * h + t] for t in range(PACK)] for h in range(2)]
         for a in range(passes1):
             w1_codes, w1_plane = quantize_dealt(w1_raw[a], "w1_%d" % a, scalar_alone,
-                                                "after_b0" if a == 0 else None, "after_b%d" % (a + 1) if a < 2 else None)
+                                                "dealt_b" if a == 1 else "dealt_a", "after_scatter0" if a == 0 else None)
             if a < passes1 - 1:
                 nc.vector.tensor_copy(v[a][:], tab_sb[a][:].indirect(offs_sb[:]))
             for h in range(2):
@@ -225,57 +229,68 @@ def tile_list_arousal_epoch_scorer_kernel(
         gain_m2 = held([P, PACK], F32, "gain_m2")
         nc.vector.tensor_scalar(out=gain_m2[:], in0=gain_sb[:], scalar1=-2.0, scalar2=None, op0=ALU.mult)
 
-        quantised = []
+        halves = [slice(HALF * h, HALF * (h + 1)) for h in range(2)]
+        a_rows, a_q = [], []
         for h in range(2):
-            epochs = slice(HALF * h, HALF * (h + 1))
-            a_rows = wide_f32([P, PACK, HALF], "a_rows")
-            for t in range(PACK):
-                sine = row_f32("sine")
-                nc.scalar.activation(out=sine[:], in_=phase[h][t][:], func=ACT.Sin, scale=0.5)
-                if h == 0 and t == 0:
+            rows = wide_f32([P, PACK, HALF], "a_rows")
+            sines = [row_f32("sine") for t in range(PACK)]
+            for step in range(PACK + 1):
+                if step < PACK:
+                    nc.scalar.activation(out=sines[step][:], in_=phase[h][step][:], func=ACT.Sin, scale=0.5)
+                if h == 0 and step == 0:
                     for a in range(passes2):
-                        signed_pass(a, last, phase[h][t])
-                    scatter(last, marked(last, phase[h][t], magnitudes[last]))
-                sine2 = row_f32("sine2")
-                nc.scalar.activation(out=sine2[:], in_=sine[:], func=ACT.Square)
-                nc.vector.tensor_scalar(
-                    out=a_rows[:, t, :], in0=sine2[:], scalar1=gain_m2[:, t : t + 1], scalar2=gain_sb[:, t : t + 1],
-                    op0=ALU.mult, op1=ALU.add,
-                )
-            a_q = interleave(nc.vector.tensor_copy, a_rows, "a_%d" % h)
-            if h == 0:
-                w4_codes, w4_plane = interleave(nc.vector.tensor_copy, w4_raw, "w4")
-            z_rows = wide_bf16([P, PACK, HALF], "z_rows")
-            for t in range(PACK):
-                nc.vector.tensor_tensor(out=z_rows[:, t, :], in0=a_rows[:, t, :], in1=placed[t][:, epochs], op=ALU.add)
-            z_q = interleave(nc.vector.tensor_copy, z_rows, "z_%d" % h)
-            quantised.append((a_q, z_q))
+                        signed_pass(a, last, phase[h][step])
+                    w4_codes, w4_plane = interleave(nc.vector.tensor_copy, w4_raw, "w4", "tab_sb2")
+                    scatter(last, marked(last, phase[h][step]))
+                if step > 0:
+                    t = step - 1
+                    nc.scalar.activation(out=sines[t][:], in_=sines[t][:], func=ACT.Square)
+                    nc.vector.tensor_scalar(
+                        out=rows[:, t, :], in0=sines[t][:], scalar1=gain_m2[:, t : t + 1],
+                        scalar2=gain_sb[:, t : t + 1], op0=ALU.mult, op1=ALU.add,
+                    )
+            a_rows.append(rows)
+            a_q.append(interleave(nc.vector.tensor_copy, rows, "a_%d" % h))
 
-        for h in range(2):
-            epochs = slice(HALF * h, HALF * (h + 1))
-            (a_codes, a_plane), (z_codes, z_plane) = quantised[h]
-            damp = []
-            for n in range(N // P):
-                cols = slice(P * n, P * (n + 1))
-                q_sum = banks[(1 + n) if h == 0 else (7 + n) % 8]
+        tiles = [slice(P * n, P * (n + 1)) for n in range(N // P)]
+
+        def damping(h):
+            a_codes, a_plane = a_q[h]
+            damp = [held([P, HALF], F32, "damp%d_%d" % (h, n)) for n in range(len(tiles))]
+            for n, cols in enumerate(tiles):
+                q_sum = banks[1 + len(tiles) * h + n]
                 nc.tensor.matmul_mx(
                     out=q_sum[:], lhsT=w5_sb[:, cols].bitcast(FP8X4), lhsT_scale=w5_planes[:, 0, cols],
                     rhs=a_codes[:].bitcast(FP8X4), rhs_scale=a_plane[:], start=True, stop=True,
                 )
-                q_abs = row_f32("q_abs")
-                nc.scalar.activation(out=q_abs[:], in_=q_sum[:], func=ACT.Abs)
-                root = row_f32("root")
-                nc.scalar.activation(out=root[:], in_=q_abs[:], func=ACT.Abs_reciprocal_sqrt, bias=1.0)
-                inverse = row_f32("inverse")
-                nc.scalar.activation(out=inverse[:], in_=root[:], func=ACT.Square)
-                damp.append(inverse)
-            for n in range(N // P):
-                cols = slice(P * n, P * (n + 1))
-                y_sum = banks[(4 + n) if h == 0 else 2 + n]
+                nc.scalar.activation(out=damp[n][:], in_=q_sum[:], func=ACT.Abs)
+            for tile in damp:
+                nc.scalar.activation(out=tile[:], in_=tile[:], func=ACT.Abs_reciprocal_sqrt, bias=1.0)
+            for tile in damp:
+                nc.scalar.activation(out=tile[:], in_=tile[:], func=ACT.Square)
+            return damp
+
+        def combined(h, copy):
+            z_rows = wide_bf16([P, PACK, HALF], "z_rows")
+            for t in range(PACK):
+                nc.vector.tensor_tensor(
+                    out=z_rows[:, t, :], in0=a_rows[h][:, t, :], in1=placed[t][:, halves[h]], op=ALU.add
+                )
+            return interleave(copy, z_rows, "z_%d" % h)
+
+        damp = [damping(0)]
+        z_q = [combined(0, nc.scalar.copy)]
+        damp.append(damping(1))
+        z_q.append(combined(1, nc.vector.tensor_copy))
+
+        for h in range(2):
+            z_codes, z_plane = z_q[h]
+            for n, cols in enumerate(tiles):
+                y_sum = banks[(7 + len(tiles) * h + n) % 8]
                 nc.tensor.matmul_mx(
                     out=y_sum[:], lhsT=w4_codes[:, cols].bitcast(FP8X4), lhsT_scale=w4_plane[:, cols],
                     rhs=z_codes[:].bitcast(FP8X4), rhs_scale=z_plane[:], start=True, stop=True,
                 )
-                score = row_f32("score")
-                nc.vector.tensor_tensor(out=score[:], in0=y_sum[:], in1=damp[n][:], op=ALU.mult)
-                nc.sync.dma_start(out=out[cols, epochs], in_=score[:])
+                score = damp[h][n]
+                nc.vector.tensor_tensor(out=score[:], in0=y_sum[:], in1=score[:], op=ALU.mult)
+                nc.sync.dma_start(out=out[cols, halves[h]], in_=score[:])

@@ -1,6 +1,7 @@
 from contextlib import ExitStack
 
 import concourse.mybir as mybir
+from concourse.masks import make_identity
 
 K, K2, T, TB, S, M, H, N = 1536, 1024, 4096, 2048, 1024, 512, 512, 384
 FLOPS = 2 * (K * H * S + 2 * K2 * H * M + 2 * H * N * S)
@@ -38,10 +39,10 @@ def tile_list_arousal_epoch_scorer_kernel(
             return keep.tile(shape, dtype, name=name, align_bytes=64)
 
         def wide_f32(shape, name):
-            return ring.tile(shape, F32, name=name, tag="wide_f32", bufs=3, align_bytes=64)
+            return ring.tile(shape, F32, name=name, tag="wide_f32", bufs=4, align_bytes=64)
 
         def row_f32(name):
-            return ring.tile([P, HALF], F32, name=name, tag="row_f32", bufs=8, align_bytes=64)
+            return ring.tile([P, HALF], F32, name=name, tag="row_f32", bufs=7, align_bytes=64)
 
         def wide_bf16(shape, name):
             return ring.tile(shape, BF16, name=name, tag="wide_bf16", bufs=4, align_bytes=64)
@@ -64,7 +65,7 @@ def tile_list_arousal_epoch_scorer_kernel(
 
         w3_raw_scales = shared([P, passes2, H], U8, "w3_raw_scales", "w3_raw_scales")
         tab2_planes = shared([P, passes2, TB], U8, "tab2_planes", "tab2_planes")
-        tab_planes = shared([P, T], U8, "tab_planes", "dealt_a")
+        tab_planes = held([P, T], U8, "tab_planes")
         w5_planes = held([P, 1, N], U8, "w5_planes")
         nc.gpsimd.memset(w3_raw_scales[:].bitcast(I32), 0)
         nc.gpsimd.memset(tab2_planes[:, 0, :].bitcast(I32), 0)
@@ -128,14 +129,11 @@ def tile_list_arousal_epoch_scorer_kernel(
         load_table(tab2_sb[0], tab2_words[0])
         load_words(nc.sync, w3_raw[:], w3_words.rearrange("a p c -> p a c"))
         load_planes_side_by_side(w3_raw_scales, w3_scales, range(QUADS))
-        wgs_sb = held([P, PACK, M], F32, "wgs_sb")
-        wgs_rows = wgs.rearrange("(p t) j -> p t j", t=PACK)
-        nc.sync.dma_start(out=wgs_sb[0:32], in_=wgs_rows)
+        wgs_raw = held([P, M], F32, "wgs_raw")
+        nc.sync.dma_start(out=wgs_raw[:], in_=wgs)
         load_planes_side_by_side(tab2_planes, tab2_scales, range(QUADS))
         load_table(tab2_sb[1], tab2_words[1])
         w2_raw = [load_weight(w2, 0, "w2_raw0"), load_weight(w2, 1, "w2_raw1", "w2_last")]
-        for q in range(1, QUADS):
-            nc.sync.dma_start(out=wgs_sb[32 * q : 32 * q + 32], in_=wgs_rows)
 
         w3_sb = held([P, passes2, 2 * H], U8, "w3_sb")
         w3_planes = shared([P, passes2, H], U8, "w3_planes", "tab2_sb0")
@@ -143,6 +141,26 @@ def tile_list_arousal_epoch_scorer_kernel(
             out=w3_sb[:].bitcast(U16).rearrange("p a (t m) -> p a t m", t=PACK),
             in_=w3_raw[:].bitcast(U16).rearrange("p a (m t) -> p a t m", t=PACK),
         )
+
+        identity = held([P, P], F32, "identity")
+        make_identity(nc, identity[:])
+        blocks = [slice(P * j, P * (j + 1)) for j in range(M // P)]
+        for cols in blocks:
+            nc.tensor.transpose(banks[2][:, cols], wgs_raw[:, cols], identity[:])
+        wgs_turned = held([P, PACK, len(blocks), P], F32, "wgs_turned")
+        by_slot = banks[2][:].rearrange("j (b p t) -> j t b p", b=len(blocks), t=PACK)
+        for t in range(PACK):
+            nc.scalar.copy(
+                out=wgs_turned[:, t].rearrange("j b (q p) -> j b q p", q=QUADS),
+                in_=by_slot[:, t].unsqueeze(2).to_broadcast([P, len(blocks), QUADS, 32]),
+            )
+        wgs_sb = []
+        for t in range(PACK):
+            bank = banks[3 + PACK * (t % 2)]
+            for j, cols in enumerate(blocks):
+                nc.tensor.transpose(bank[:, cols], wgs_turned[:, t, j, :], identity[:])
+            wgs_sb.append(shared([P, M], F32, "wgs_sb%d" % t, "wgs_sb%d" % t))
+            nc.scalar.copy(out=wgs_sb[t][:], in_=bank[:])
 
         v2 = [held([P, M], U32, "v2_0"), shared([P, M], U32, "v2_1", "tab2_planes")]
         v2_planes = [held([P, M], U8, "v2_plane%d" % a) for a in range(passes2)]
@@ -154,13 +172,11 @@ def tile_list_arousal_epoch_scorer_kernel(
         for a in range(passes2):
             nc.vector.tensor_copy(v2_planes[a][:], tab2_planes[:, a, :].indirect(offs2_sb[:]))
         nc.vector.tensor_copy(v2[1][:], tab2_sb[1][:].indirect(offs2_sb[:]))
-        v_planes = shared([P, S], U8, "v_planes", "tab2_sb1")
-        nc.vector.tensor_copy(v_planes[:], tab_planes[:].indirect(offs_sb[:]))
         scalar_alone = [(nc.scalar.copy, slice(0, P))]
-        both = [(nc.scalar.copy, slice(0, P // 2)), (nc.vector.tensor_copy, slice(P // 2, P))]
+        both = [(nc.vector.tensor_copy, slice(0, P))]
         w2_q = [
             quantize_dealt(w2_raw[0], "w2_0", scalar_alone, "dealt_b", None, "w3_raw_scales"),
-            quantize_dealt(w2_raw[1], "w2_1", both, "dealt_a"),
+            quantize_dealt(w2_raw[1], "w2_1", both, "tab2_sb1"),
         ]
 
         w1_raw = []
@@ -195,7 +211,7 @@ def tile_list_arousal_epoch_scorer_kernel(
             return b_row
 
         def scatter(t, b_row):
-            nc.vector.tensor_tensor(placed[t][:].indirect(pos_sb[:]), b_row[:], wgs_sb[:, t, :], ALU.mult)
+            nc.vector.tensor_tensor(placed[t][:].indirect(pos_sb[:]), b_row[:], wgs_sb[t][:], ALU.mult)
 
         last = PACK - 1
         for t in range(PACK):
@@ -207,11 +223,13 @@ def tile_list_arousal_epoch_scorer_kernel(
             if t < last:
                 scatter(t, marked(t, banks[PACK + t]))
 
+        v_planes = shared([P, S], U8, "v_planes", "wgs_sb1")
+        nc.vector.tensor_copy(v_planes[:], tab_planes[:].indirect(offs_sb[:]))
         v = [shared([P, S], U32, "v_%d" % a, "after_scatter%d" % min(a + 1, 2) if a < 2 else "v_last") for a in range(passes1)]
         phase = [[banks[PACK * h + t] for t in range(PACK)] for h in range(2)]
         for a in range(passes1):
             w1_codes, w1_plane = quantize_dealt(w1_raw[a], "w1_%d" % a, scalar_alone,
-                                                "dealt_b" if a == 1 else "dealt_a", "after_scatter0" if a == 0 else None)
+                                                "dealt_b" if a == 1 else "tab2_sb1", "after_scatter0" if a == 0 else None)
             if a < passes1 - 1:
                 nc.vector.tensor_copy(v[a][:], tab_sb[a][:].indirect(offs_sb[:]))
             for h in range(2):
@@ -254,20 +272,22 @@ def tile_list_arousal_epoch_scorer_kernel(
 
         tiles = [slice(P * n, P * (n + 1)) for n in range(N // P)]
 
+        scores = shared([P, 2 * len(tiles), HALF], F32, "scores", "tab_sb0")
+
         def damping(h):
             a_codes, a_plane = a_q[h]
-            damp = [held([P, HALF], F32, "damp%d_%d" % (h, n)) for n in range(len(tiles))]
+            damp = [scores[:, len(tiles) * h + n, :] for n in range(len(tiles))]
             for n, cols in enumerate(tiles):
                 q_sum = banks[1 + len(tiles) * h + n]
                 nc.tensor.matmul_mx(
                     out=q_sum[:], lhsT=w5_sb[:, cols].bitcast(FP8X4), lhsT_scale=w5_planes[:, 0, cols],
                     rhs=a_codes[:].bitcast(FP8X4), rhs_scale=a_plane[:], start=True, stop=True,
                 )
-                nc.scalar.activation(out=damp[n][:], in_=q_sum[:], func=ACT.Abs)
+                nc.scalar.activation(out=damp[n], in_=q_sum[:], func=ACT.Abs)
             for tile in damp:
-                nc.scalar.activation(out=tile[:], in_=tile[:], func=ACT.Abs_reciprocal_sqrt, bias=1.0)
+                nc.scalar.activation(out=tile, in_=tile, func=ACT.Abs_reciprocal_sqrt, bias=1.0)
             for tile in damp:
-                nc.scalar.activation(out=tile[:], in_=tile[:], func=ACT.Square)
+                nc.scalar.activation(out=tile, in_=tile, func=ACT.Square)
             return damp
 
         def combined(h, copy):
@@ -292,5 +312,5 @@ def tile_list_arousal_epoch_scorer_kernel(
                     rhs=z_codes[:].bitcast(FP8X4), rhs_scale=z_plane[:], start=True, stop=True,
                 )
                 score = damp[h][n]
-                nc.vector.tensor_tensor(out=score[:], in0=y_sum[:], in1=score[:], op=ALU.mult)
-                nc.sync.dma_start(out=out[cols, halves[h]], in_=score[:])
+                nc.vector.tensor_tensor(out=score, in0=y_sum[:], in1=score, op=ALU.mult)
+                nc.sync.dma_start(out=out[cols, halves[h]], in_=score)

@@ -3,8 +3,10 @@ from contextlib import ExitStack
 import concourse.mybir as mybir
 from concourse.masks import make_identity
 
-K, K2, T, TB, S, M, H, N = 1536, 1024, 4096, 2048, 1024, 512, 512, 384
-FLOPS = 2 * (K * H * S + 2 * K2 * H * M + 2 * H * N * S)
+K, K2, H, N = 1536, 1024, 512, 384
+TABLE, TABLE2 = 4096, 2048
+EPOCHS, MARKED = 1024, 512
+FLOPS = 2 * (K * H * EPOCHS + 2 * K2 * H * MARKED + 2 * H * N * EPOCHS)
 
 F32 = mybir.dt.float32
 BF16 = mybir.dt.bfloat16
@@ -18,9 +20,15 @@ ALU = mybir.AluOpType
 ACT = mybir.ActivationFunctionType
 
 P = 128
-PACK = 4
-QUADS = 4
+SLOTS = 4
+K_PASS = P * SLOTS
+QUADS, QUAD = 4, 32
+SCALE_ROWS = 4
+GROUP = 16
 HALF = 512
+BANKS = 8
+PASSES, PASSES2 = K // K_PASS, K2 // K_PASS
+EARLY = SLOTS // 2
 
 
 def tile_list_arousal_epoch_scorer_kernel(
@@ -28,7 +36,6 @@ def tile_list_arousal_epoch_scorer_kernel(
     wgs, w4, w5_words, w5_scales, offs, offs2, pos1, out,
 ):
     nc = tc.nc
-    passes1, passes2 = K // 512, K2 // 512
 
     with ExitStack() as ctx:
         keep = ctx.enter_context(tc.tile_pool(name="keep", bufs=1))
@@ -38,279 +45,292 @@ def tile_list_arousal_epoch_scorer_kernel(
         def held(shape, dtype, name):
             return keep.tile(shape, dtype, name=name, align_bytes=64)
 
+        def in_buffer(buffer, shape, dtype, name):
+            return ring.tile(shape, dtype, name=name, tag=buffer, bufs=1, align_bytes=64)
+
         def wide_f32(shape, name):
             return ring.tile(shape, F32, name=name, tag="wide_f32", bufs=4, align_bytes=64)
 
-        def row_f32(name):
-            return ring.tile([P, HALF], F32, name=name, tag="row_f32", bufs=7, align_bytes=64)
+        def sine_row():
+            return ring.tile([P, HALF], F32, name="sine", tag="sine", bufs=7, align_bytes=64)
 
         def wide_bf16(shape, name):
             return ring.tile(shape, BF16, name=name, tag="wide_bf16", bufs=4, align_bytes=64)
 
-        banks = [psum.tile([P, HALF], F32, name="bank%d" % i) for i in range(8)]
+        banks = [psum.tile([P, HALF], F32, name="bank%d" % i) for i in range(BANKS)]
 
-        def shared(shape, dtype, name, tag):
-            return ring.tile(shape, dtype, name=name, tag=tag, bufs=1, align_bytes=64)
+        def load_bytes(queue, tile, source):
+            queue.dma_start(out=tile.bitcast(I32), in_=source.bitcast(I32))
 
-        def load_words(queue, tile, words):
-            queue.dma_start(out=tile.bitcast(I32), in_=words.bitcast(I32))
-
-        def load_planes_side_by_side(tile, scales, quadrants):
+        def load_plane_rows(tile, scales, quadrants):
             for q in quadrants:
-                load_words(nc.sync, tile[32 * q : 32 * q + 4], scales[:, 4 * q : 4 * q + 4, :].rearrange("a r c -> r a c"))
-
-        offs_sb = keep.tile([P, S // 16], U16, name="offs_sb")
-        offs2_sb = keep.tile([P, M // 16], U16, name="offs2_sb")
-        pos_sb = keep.tile([P, M // 16], U16, name="pos_sb")
-
-        w3_raw_scales = shared([P, passes2, H], U8, "w3_raw_scales", "w3_raw_scales")
-        tab2_planes = shared([P, passes2, TB], U8, "tab2_planes", "tab2_planes")
-        tab_planes = held([P, T], U8, "tab_planes")
-        w5_planes = held([P, 1, N], U8, "w5_planes")
-        nc.gpsimd.memset(w3_raw_scales[:].bitcast(I32), 0)
-        nc.gpsimd.memset(tab2_planes[:, 0, :].bitcast(I32), 0)
-        nc.vector.memset(tab2_planes[:, 1, :].bitcast(I32), 0)
-        for tile in (tab_planes, w5_planes):
-            nc.vector.memset(tile[:].bitcast(I32), 0)
-        placed = [held([P, S], F32, "placed%d" % t) for t in range(PACK)]
-        for t in range(PACK):
-            nc.vector.memset(placed[t][:], 0.0)
-
-        tab2_sb = [shared([P, TB], U32, "tab2_sb%d" % a, "tab2_sb%d" % a) for a in range(passes2)]
-        tab_sb = [ring.tile([P, T], U32, name="tab_sb%d" % a, tag="tab_sb%d" % a, bufs=1, align_bytes=64) for a in range(passes1)]
-        w3_raw = held([P, passes2, 2 * H], U8, "w3_raw")
+                rows = scales[:, SCALE_ROWS * q : SCALE_ROWS * (q + 1), :]
+                load_bytes(nc.sync, tile[QUAD * q : QUAD * q + SCALE_ROWS], rows.rearrange("g i c -> i g c"))
 
         def load_table(tile, words):
-            load_words(nc.sync, tile[:], words.rearrange("p t i -> p (t i)"))
+            load_bytes(nc.sync, tile[:], words.rearrange("p c t -> p (c t)"))
 
-        def load_weight(w, a, name, tag=None):
-            shape = [P, PACK, w.shape[1]]
-            raw = shared(shape, F32, name, tag) if tag else wide_f32(shape, name)
-            nc.sync.dma_start(out=raw[:], in_=w[512 * a : 512 * (a + 1), :].rearrange("(p j) c -> p j c", j=PACK))
-            return raw
+        def load_weight(tile, w, g):
+            rows = w[K_PASS * g : K_PASS * (g + 1), :]
+            nc.sync.dma_start(out=tile[:], in_=rows.rearrange("(p t) c -> p t c", t=SLOTS))
+            return tile
 
-        def quantize(grouped, name, tag=None, plane_tag=None):
-            width = grouped.shape[1] // PACK
-            codes = shared([P, width], U32, name + "_codes", tag or name)
-            plane = shared([P, width], U8, name + "_plane", plane_tag or name + "_plane")
-            nc.vector.quantize_mx(out=codes[:].bitcast(FP8X4), scales=plane[:], in_=grouped[:])
+        def round_dealt(copy, raw, buffer, name):
+            rounded = in_buffer(buffer, [P, SLOTS * H], BF16, name)
+            copy(
+                out=rounded[:].rearrange("p (s m t) -> p m s t", s=SLOTS, t=SLOTS),
+                in_=raw[:].rearrange("p t (m s) -> p m s t", s=SLOTS),
+            )
+            return rounded
+
+        def interleave(rounded, rows):
+            nc.vector.tensor_copy(
+                out=rounded[:].rearrange("p (c t) -> p c t", t=SLOTS), in_=rows[:].rearrange("p t c -> p c t")
+            )
+            return rounded
+
+        def quantize(rounded, name, codes_buffer=None, plane_buffer=None):
+            width = rounded.shape[1] // SLOTS
+            codes = in_buffer(codes_buffer or name + "_codes", [P, width], U32, name + "_codes")
+            plane = in_buffer(plane_buffer or name + "_plane", [P, width], U8, name + "_plane")
+            nc.vector.quantize_mx(out=codes[:].bitcast(FP8X4), scales=plane[:], in_=rounded[:])
             return codes, plane
 
-        def quantize_dealt(raw, name, shares, bf16_tag=None, codes_tag=None, plane_tag=None):
-            if bf16_tag:
-                grouped = shared([P, PACK * H], BF16, name + "_bf16", bf16_tag)
-            else:
-                grouped = wide_bf16([P, PACK * H], name + "_bf16")
-            dealt = grouped[:].rearrange("p (t m j) -> p m t j", t=PACK, j=PACK)
-            given = raw[:].rearrange("p j (m t) -> p m t j", t=PACK)
-            for copy, rows in shares:
-                copy(out=dealt[:, rows], in_=given[:, rows])
-            return quantize(grouped, name, codes_tag, plane_tag)
+        def gather(picked, window, offsets):
+            nc.vector.tensor_copy(picked, window.indirect(offsets))
 
-        def interleave(copy, rows, name, bf16_tag=None):
-            width = rows.shape[2]
-            if bf16_tag:
-                grouped = shared([P, PACK * width], BF16, name + "_bf16", bf16_tag)
-            else:
-                grouped = wide_bf16([P, PACK * width], name + "_bf16")
-            copy(
-                out=grouped[:].rearrange("p (c t) -> p c t", t=PACK),
-                in_=rows[:].rearrange("p t c -> p c t"),
-            )
-            return quantize(grouped, name)
+        blocks = [slice(P * i, P * (i + 1)) for i in range(SLOTS)]
+        halves = [slice(HALF * h, HALF * (h + 1)) for h in range(EPOCHS // HALF)]
+
+        offs_sb = keep.tile([P, EPOCHS // GROUP], U16, name="offs_sb")
+        offs2_sb = keep.tile([P, MARKED // GROUP], U16, name="offs2_sb")
+        pos_sb = keep.tile([P, MARKED // GROUP], U16, name="pos_sb")
+
+        w3_given_planes = in_buffer("w3_given_planes", [P, PASSES2, H], U8, "w3_given_planes")
+        tab2_planes = in_buffer("tab2_planes", [P, PASSES2, TABLE2], U8, "tab2_planes")
+        tab_planes = in_buffer("tab_planes", [P, TABLE], U8, "tab_planes")
+        w5_plane = held([P, 1, N], U8, "w5_plane")
+        nc.gpsimd.memset(w3_given_planes[:].bitcast(I32), 0)
+        nc.gpsimd.memset(tab2_planes[:, 0, :].bitcast(I32), 0)
+        nc.vector.memset(tab2_planes[:, 1, :].bitcast(I32), 0)
+        for tile in (tab_planes, w5_plane):
+            nc.vector.memset(tile[:].bitcast(I32), 0)
+        placed = [held([P, EPOCHS], F32, "placed%d" % t) for t in range(SLOTS)]
+        for tile in placed:
+            nc.vector.memset(tile[:], 0.0)
+
+        tab2_sb = [in_buffer("tab2_%d" % g, [P, TABLE2], U32, "tab2_sb") for g in range(PASSES2)]
+        tab_sb = [in_buffer("tab_%d" % g, [P, TABLE], U32, "tab_sb") for g in range(PASSES)]
 
         for q in range(QUADS):
-            load_words(nc.gpsimd, tab_planes[32 * q : 32 * q + 4 * passes1, :], tab_scales[:, 4 * q : 4 * q + 4, :])
+            load_bytes(
+                nc.gpsimd, tab_planes[QUAD * q : QUAD * q + SCALE_ROWS * PASSES, :],
+                tab_scales[:, SCALE_ROWS * q : SCALE_ROWS * (q + 1), :],
+            )
         nc.sync.dma_start(offs2_sb[:], offs2)
         nc.sync.dma_start(offs_sb[:], offs)
         nc.sync.dma_start(pos_sb[:], pos1)
-        gain_sb = held([P, PACK], F32, "gain_sb")
-        nc.sync.dma_start(out=gain_sb[:], in_=gain.rearrange("(p t) -> p t", t=PACK))
+        gain_sb = held([P, SLOTS], F32, "gain_sb")
+        nc.sync.dma_start(out=gain_sb[:], in_=gain.rearrange("(p t) -> p t", t=SLOTS))
         load_table(tab2_sb[0], tab2_words[0])
-        load_words(nc.sync, w3_raw[:], w3_words.rearrange("a p c -> p a c"))
-        load_planes_side_by_side(w3_raw_scales, w3_scales, range(QUADS))
-        wgs_raw = held([P, M], F32, "wgs_raw")
-        nc.sync.dma_start(out=wgs_raw[:], in_=wgs)
-        load_planes_side_by_side(tab2_planes, tab2_scales, range(QUADS))
+        wgs_given = held([P, MARKED], F32, "wgs_given")
+        nc.sync.dma_start(out=wgs_given[:], in_=wgs)
+        w3_given = held([P, PASSES2, 2 * H], U8, "w3_given")
+        load_bytes(nc.sync, w3_given[:], w3_words.rearrange("g p c -> p g c"))
+        load_plane_rows(w3_given_planes, w3_scales, range(QUADS))
         load_table(tab2_sb[1], tab2_words[1])
-        w2_raw = [load_weight(w2, 0, "w2_raw0"), load_weight(w2, 1, "w2_raw1", "w2_last")]
+        load_plane_rows(tab2_planes, tab2_scales, range(QUADS))
+        w2_given = [
+            load_weight(in_buffer("w2_first", [P, SLOTS, H], F32, "w2_given"), w2, 0),
+            load_weight(wide_f32([P, SLOTS, H], "w2_given"), w2, 1),
+        ]
 
-        w3_sb = held([P, passes2, 2 * H], U8, "w3_sb")
-        w3_planes = shared([P, passes2, H], U8, "w3_planes", "tab2_sb0")
+        w3_sb = held([P, PASSES2, 2 * H], U8, "w3_sb")
         nc.scalar.copy(
-            out=w3_sb[:].bitcast(U16).rearrange("p a (t m) -> p a t m", t=PACK),
-            in_=w3_raw[:].bitcast(U16).rearrange("p a (m t) -> p a t m", t=PACK),
+            out=w3_sb[:].bitcast(U16).rearrange("p g (s m) -> p g s m", s=SLOTS),
+            in_=w3_given[:].bitcast(U16).rearrange("p g (m s) -> p g s m", s=SLOTS),
         )
 
         identity = held([P, P], F32, "identity")
         make_identity(nc, identity[:])
-        blocks = [slice(P * j, P * (j + 1)) for j in range(M // P)]
+        turn_bank = banks[2]
         for cols in blocks:
-            nc.tensor.transpose(banks[2][:, cols], wgs_raw[:, cols], identity[:])
-        wgs_turned = held([P, PACK, len(blocks), P], F32, "wgs_turned")
-        by_slot = banks[2][:].rearrange("j (b p t) -> j t b p", b=len(blocks), t=PACK)
-        for t in range(PACK):
+            nc.tensor.transpose(turn_bank[:, cols], wgs_given[:, cols], identity[:])
+        wgs_turned = held([P, SLOTS, len(blocks), P], F32, "wgs_turned")
+        by_slot = turn_bank[:].rearrange("j (b p t) -> j t b p", b=len(blocks), t=SLOTS)
+        for t in range(SLOTS):
             nc.scalar.copy(
                 out=wgs_turned[:, t].rearrange("j b (q p) -> j b q p", q=QUADS),
-                in_=by_slot[:, t].unsqueeze(2).to_broadcast([P, len(blocks), QUADS, 32]),
+                in_=by_slot[:, t].unsqueeze(2).to_broadcast([P, len(blocks), QUADS, QUAD]),
             )
-        wgs_sb = []
-        for t in range(PACK):
-            bank = banks[3 + PACK * (t % 2)]
-            for j, cols in enumerate(blocks):
-                nc.tensor.transpose(bank[:, cols], wgs_turned[:, t, j, :], identity[:])
-            wgs_sb.append(shared([P, M], F32, "wgs_sb%d" % t, "wgs_sb%d" % t))
+        wgs_sb = [held([P, MARKED], F32, "wgs_sb%d" % t) for t in range(SLOTS)]
+
+        def turn_wgs_back(t, bank):
+            for i, cols in enumerate(blocks):
+                nc.tensor.transpose(bank[:, cols], wgs_turned[:, t, i, :], identity[:])
             nc.scalar.copy(out=wgs_sb[t][:], in_=bank[:])
 
-        v2 = [held([P, M], U32, "v2_0"), shared([P, M], U32, "v2_1", "tab2_planes")]
-        v2_planes = [held([P, M], U8, "v2_plane%d" % a) for a in range(passes2)]
-        nc.vector.tensor_copy(v2[0][:], tab2_sb[0][:].indirect(offs2_sb[:]))
+        for t in range(EARLY):
+            turn_wgs_back(t, banks[BANKS - EARLY + t])
+
+        v2 = [held([P, MARKED], U32, "v2_first")]
+        gather(v2[0][:], tab2_sb[0][:], offs2_sb[:])
+        w3_planes = in_buffer("tab2_0", [P, PASSES2, H], U8, "w3_planes")
         nc.vector.tensor_copy(
-            out=w3_planes[:].rearrange("p a (t m) -> p a t m", t=PACK),
-            in_=w3_raw_scales[:].rearrange("p a (m t) -> p a t m", t=PACK),
+            out=w3_planes[:].rearrange("p g (s m) -> p g s m", s=SLOTS),
+            in_=w3_given_planes[:].rearrange("p g (m s) -> p g s m", s=SLOTS),
         )
-        for a in range(passes2):
-            nc.vector.tensor_copy(v2_planes[a][:], tab2_planes[:, a, :].indirect(offs2_sb[:]))
-        nc.vector.tensor_copy(v2[1][:], tab2_sb[1][:].indirect(offs2_sb[:]))
-        scalar_alone = [(nc.scalar.copy, slice(0, P))]
-        both = [(nc.vector.tensor_copy, slice(0, P))]
-        w2_q = [
-            quantize_dealt(w2_raw[0], "w2_0", scalar_alone, "dealt_b", None, "w3_raw_scales"),
-            quantize_dealt(w2_raw[1], "w2_1", both, "tab2_sb1"),
+        v2_planes = [held([P, MARKED], U8, "v2_plane%d" % g) for g in range(PASSES2)]
+        for g in range(PASSES2):
+            gather(v2_planes[g][:], tab2_planes[:, g, :], offs2_sb[:])
+        v2.append(in_buffer("tab2_planes", [P, MARKED], U32, "v2_last"))
+        gather(v2[1][:], tab2_sb[1][:], offs2_sb[:])
+        w2_rounded = [
+            round_dealt(nc.scalar.copy, w2_given[0], "rounded", "w2_rounded"),
+            round_dealt(nc.vector.tensor_copy, w2_given[1], "tab2_1", "w2_rounded"),
         ]
+        w2_q = [quantize(w2_rounded[0], "w2_0", plane_buffer="w3_given_planes"), quantize(w2_rounded[1], "w2_1")]
 
-        w1_raw = []
-        for a in range(passes1):
-            w1_raw.append(load_weight(w1, a, "w1_raw%d" % a))
-            load_table(tab_sb[a], tab_words[a])
-        w4_raw = load_weight(w4, 0, "w4_raw")
+        w1_given = []
+        for g in range(PASSES):
+            w1_given.append(load_weight(wide_f32([P, SLOTS, H], "w1_given"), w1, g))
+            load_table(tab_sb[g], tab_words[g])
+        w4_given = load_weight(wide_f32([P, SLOTS, N], "w4_given"), w4, 0)
         w5_sb = held([P, N], U32, "w5_sb")
-        load_words(nc.sync, w5_sb[:], w5_words[0].rearrange("p c i -> p (c i)"))
-        load_planes_side_by_side(w5_planes, w5_scales, range(QUADS))
+        load_table(w5_sb, w5_words[0])
+        load_plane_rows(w5_plane, w5_scales, range(QUADS))
 
-        def magnitude_pass(a, t, m2):
+        def magnitude_pass(g, t, bank):
             nc.tensor.matmul_mx(
-                out=m2[:], lhsT=w3_sb[:, a, 2 * P * t : 2 * P * (t + 1)].bitcast(FP4X4),
-                lhsT_scale=w3_planes[:, a, P * t : P * (t + 1)], rhs=v2[a][:].bitcast(FP8X4),
-                rhs_scale=v2_planes[a][:], start=(a == 0), stop=(a == passes2 - 1),
+                out=bank[:], lhsT=w3_sb[:, g, 2 * P * t : 2 * P * (t + 1)].bitcast(FP4X4),
+                lhsT_scale=w3_planes[:, g, blocks[t]], rhs=v2[g][:].bitcast(FP8X4), rhs_scale=v2_planes[g][:],
+                start=(g == 0), stop=(g == PASSES2 - 1),
             )
 
-        def signed_pass(a, t, m1):
-            cols = slice(P * t, P * (t + 1))
+        def signed_pass(g, t, bank):
+            codes, plane = w2_q[g]
             nc.tensor.matmul_mx(
-                out=m1[:], lhsT=w2_q[a][0][:, cols].bitcast(FP8X4), lhsT_scale=w2_q[a][1][:, cols],
-                rhs=v2[a][:].bitcast(FP8X4), rhs_scale=v2_planes[a][:],
-                start=(a == 0), stop=(a == passes2 - 1),
+                out=bank[:], lhsT=codes[:, blocks[t]].bitcast(FP8X4), lhsT_scale=plane[:, blocks[t]],
+                rhs=v2[g][:].bitcast(FP8X4), rhs_scale=v2_planes[g][:],
+                start=(g == 0), stop=(g == PASSES2 - 1),
             )
 
-        magnitudes = shared([P, PACK, M], F32, "magnitudes", "w2_last")
+        magnitudes = in_buffer("w2_first", [P, SLOTS, MARKED], F32, "magnitudes")
 
-        def marked(t, m1):
-            b_row = shared([P, M], F32, "b_row%d" % t, "after_scatter%d" % t)
-            nc.vector.tensor_tensor(out=b_row[:], in0=m1[:], in1=magnitudes[:, t, :], op=ALU.mult)
-            return b_row
+        def place(t, signed_bank):
+            b_rows = in_buffer("b_%d" % t, [P, MARKED], F32, "b_rows")
+            nc.vector.tensor_tensor(out=b_rows[:], in0=signed_bank[:], in1=magnitudes[:, t, :], op=ALU.mult)
+            nc.vector.tensor_tensor(placed[t][:].indirect(pos_sb[:]), b_rows[:], wgs_sb[t][:], ALU.mult)
 
-        def scatter(t, b_row):
-            nc.vector.tensor_tensor(placed[t][:].indirect(pos_sb[:]), b_row[:], wgs_sb[t][:], ALU.mult)
-
-        last = PACK - 1
-        for t in range(PACK):
-            for a in range(passes2):
-                magnitude_pass(a, t, banks[t % 2])
-                if t < last:
-                    signed_pass(a, t, banks[PACK + t])
+        for t in range(SLOTS):
+            for g in range(PASSES2):
+                magnitude_pass(g, t, banks[t % 2])
+                if t < EARLY:
+                    signed_pass(g, t, banks[SLOTS + t])
             nc.scalar.activation(out=magnitudes[:, t, :], in_=banks[t % 2][:], func=ACT.Abs)
-            if t < last:
-                scatter(t, marked(t, banks[PACK + t]))
+            if t < EARLY:
+                place(t, banks[SLOTS + t])
+        for t in range(EARLY, SLOTS):
+            turn_wgs_back(t, banks[t % 2])
 
-        v_planes = shared([P, S], U8, "v_planes", "wgs_sb1")
-        nc.vector.tensor_copy(v_planes[:], tab_planes[:].indirect(offs_sb[:]))
-        v = [shared([P, S], U32, "v_%d" % a, "after_scatter%d" % min(a + 1, 2) if a < 2 else "v_last") for a in range(passes1)]
-        phase = [[banks[PACK * h + t] for t in range(PACK)] for h in range(2)]
-        for a in range(passes1):
-            w1_codes, w1_plane = quantize_dealt(w1_raw[a], "w1_%d" % a, scalar_alone,
-                                                "dealt_b" if a == 1 else "tab2_sb1", "after_scatter0" if a == 0 else None)
-            if a < passes1 - 1:
-                nc.vector.tensor_copy(v[a][:], tab_sb[a][:].indirect(offs_sb[:]))
-            for h in range(2):
-                epochs = slice(HALF * h, HALF * (h + 1))
-                if a == passes1 - 1:
-                    nc.vector.tensor_copy(v[a][:, epochs], tab_sb[a][:].indirect(offs_sb[:, 32 * h : 32 * (h + 1)]))
-                for t in range(PACK):
-                    cols = slice(P * t, P * (t + 1))
+        rounded_buffers = ("tab2_1", "rounded", "tab2_1")
+        codes_buffers = ("b_0", None, None)
+        picked_buffers = ("b_1", "tab_planes", "v_last")
+        w1_q, v = [], []
+        for g in range(PASSES):
+            rounded = round_dealt(nc.scalar.copy, w1_given[g], rounded_buffers[g], "w1_rounded")
+            w1_q.append(quantize(rounded, "w1_%d" % g, codes_buffer=codes_buffers[g]))
+            v.append(in_buffer(picked_buffers[g], [P, EPOCHS], U32, "v"))
+            if g < PASSES - 1:
+                gather(v[g][:], tab_sb[g][:], offs_sb[:])
+            else:
+                for epochs in halves:
+                    gather(v[g][:, epochs], tab_sb[g][:], offs_sb[:, epochs.start // GROUP : epochs.stop // GROUP])
+            if g == 0:
+                v_planes = in_buffer("tab_0", [P, EPOCHS], U8, "v_planes")
+                gather(v_planes[:], tab_planes[:], offs_sb[:])
+
+        phase = [[banks[SLOTS * h + t] for t in range(SLOTS)] for h in range(len(halves))]
+        for h, epochs in enumerate(halves):
+            for g in range(PASSES):
+                codes, plane = w1_q[g]
+                for t in range(SLOTS):
                     nc.tensor.matmul_mx(
-                        out=phase[h][t][:], lhsT=w1_codes[:, cols].bitcast(FP8X4), lhsT_scale=w1_plane[:, cols],
-                        rhs=v[a][:, epochs].bitcast(FP8X4), rhs_scale=v_planes[4 * a :, epochs],
-                        start=(a == 0), stop=(a == passes1 - 1),
+                        out=phase[h][t][:], lhsT=codes[:, blocks[t]].bitcast(FP8X4), lhsT_scale=plane[:, blocks[t]],
+                        rhs=v[g][:, epochs].bitcast(FP8X4), rhs_scale=v_planes[SCALE_ROWS * g :, epochs],
+                        start=(g == 0), stop=(g == PASSES - 1),
                     )
 
-        gain_m2 = held([P, PACK], F32, "gain_m2")
-        nc.vector.tensor_scalar(out=gain_m2[:], in0=gain_sb[:], scalar1=-2.0, scalar2=None, op0=ALU.mult)
+        minus_two_gain = held([P, SLOTS], F32, "minus_two_gain")
+        nc.vector.tensor_scalar(out=minus_two_gain[:], in0=gain_sb[:], scalar1=-2.0, scalar2=None, op0=ALU.mult)
 
-        halves = [slice(HALF * h, HALF * (h + 1)) for h in range(2)]
+        def apply_gain(rows, squares, t):
+            nc.scalar.activation(
+                out=rows[:, t, :], in_=squares[t][:], func=ACT.Identity,
+                scale=minus_two_gain[:, t : t + 1], bias=gain_sb[:, t : t + 1],
+            )
+
         a_rows, a_q = [], []
-        for h in range(2):
-            rows = wide_f32([P, PACK, HALF], "a_rows")
-            sines = [row_f32("sine") for t in range(PACK)]
-            for step in range(PACK + 1):
-                if step < PACK:
+        for h in range(len(halves)):
+            rows = wide_f32([P, SLOTS, HALF], "a_rows")
+            sines = [sine_row() for t in range(SLOTS)]
+            for step in range(SLOTS + 1):
+                if step < SLOTS:
                     nc.scalar.activation(out=sines[step][:], in_=phase[h][step][:], func=ACT.Sin, scale=0.5)
                 if h == 0 and step == 0:
-                    for a in range(passes2):
-                        signed_pass(a, last, phase[h][step])
-                    w4_codes, w4_plane = interleave(nc.vector.tensor_copy, w4_raw, "w4", "tab_sb2")
-                    scatter(last, marked(last, phase[h][step]))
+                    w4_rounded = in_buffer("tab_2", [P, SLOTS * N], BF16, "w4_rounded")
+                    w4_codes, w4_plane = quantize(interleave(w4_rounded, w4_given), "w4")
+                if h == 0 and step < SLOTS - EARLY:
+                    for g in range(PASSES2):
+                        signed_pass(g, EARLY + step, phase[h][step])
+                    place(EARLY + step, phase[h][step])
                 if step > 0:
-                    t = step - 1
-                    nc.scalar.activation(out=sines[t][:], in_=sines[t][:], func=ACT.Square)
-                    nc.vector.tensor_scalar(
-                        out=rows[:, t, :], in0=sines[t][:], scalar1=gain_m2[:, t : t + 1],
-                        scalar2=gain_sb[:, t : t + 1], op0=ALU.mult, op1=ALU.add,
-                    )
+                    nc.scalar.activation(out=sines[step - 1][:], in_=sines[step - 1][:], func=ACT.Square)
+                if step > 1:
+                    apply_gain(rows, sines, step - 2)
+            apply_gain(rows, sines, SLOTS - 1)
             a_rows.append(rows)
-            a_q.append(interleave(nc.vector.tensor_copy, rows, "a_%d" % h))
+            a_q.append(quantize(interleave(wide_bf16([P, SLOTS * HALF], "a_rounded"), rows), "a_%d" % h))
 
-        tiles = [slice(P * n, P * (n + 1)) for n in range(N // P)]
+        out_blocks = blocks[: N // P]
+        scores = in_buffer("tab_0", [P, len(halves), len(out_blocks), HALF], F32, "scores")
 
-        scores = shared([P, 2 * len(tiles), HALF], F32, "scores", "tab_sb0")
-
-        def damping(h):
-            a_codes, a_plane = a_q[h]
-            damp = [scores[:, len(tiles) * h + n, :] for n in range(len(tiles))]
-            for n, cols in enumerate(tiles):
-                q_sum = banks[1 + len(tiles) * h + n]
+        def damp(h):
+            codes, plane = a_q[h]
+            pieces = [scores[:, h, n, :] for n in range(len(out_blocks))]
+            for n, cols in enumerate(out_blocks):
+                bank = banks[1 + len(out_blocks) * h + n]
                 nc.tensor.matmul_mx(
-                    out=q_sum[:], lhsT=w5_sb[:, cols].bitcast(FP8X4), lhsT_scale=w5_planes[:, 0, cols],
-                    rhs=a_codes[:].bitcast(FP8X4), rhs_scale=a_plane[:], start=True, stop=True,
+                    out=bank[:], lhsT=w5_sb[:, cols].bitcast(FP8X4), lhsT_scale=w5_plane[:, 0, cols],
+                    rhs=codes[:].bitcast(FP8X4), rhs_scale=plane[:], start=True, stop=True,
                 )
-                nc.scalar.activation(out=damp[n], in_=q_sum[:], func=ACT.Abs)
-            for tile in damp:
-                nc.scalar.activation(out=tile, in_=tile, func=ACT.Abs_reciprocal_sqrt, bias=1.0)
-            for tile in damp:
-                nc.scalar.activation(out=tile, in_=tile, func=ACT.Square)
-            return damp
+                nc.scalar.activation(out=pieces[n], in_=bank[:], func=ACT.Abs)
+            for piece in pieces:
+                nc.scalar.activation(out=piece, in_=piece, func=ACT.Abs_reciprocal_sqrt, bias=1.0)
+            for piece in pieces:
+                nc.scalar.activation(out=piece, in_=piece, func=ACT.Square)
 
-        def combined(h, copy):
-            z_rows = wide_bf16([P, PACK, HALF], "z_rows")
-            for t in range(PACK):
+        def quantize_z(h):
+            z_rows = wide_bf16([P, SLOTS, HALF], "z_rows")
+            for t in range(SLOTS):
                 nc.vector.tensor_tensor(
                     out=z_rows[:, t, :], in0=a_rows[h][:, t, :], in1=placed[t][:, halves[h]], op=ALU.add
                 )
-            return interleave(copy, z_rows, "z_%d" % h)
+            return quantize(interleave(wide_bf16([P, SLOTS * HALF], "z_rounded"), z_rows), "z_%d" % h)
 
-        damp = [damping(0)]
-        z_q = [combined(0, nc.scalar.copy)]
-        damp.append(damping(1))
-        z_q.append(combined(1, nc.vector.tensor_copy))
+        z_q = []
+        for h in range(len(halves)):
+            damp(h)
+            z_q.append(quantize_z(h))
 
-        for h in range(2):
-            z_codes, z_plane = z_q[h]
-            for n, cols in enumerate(tiles):
-                y_sum = banks[(7 + len(tiles) * h + n) % 8]
+        for h, epochs in enumerate(halves):
+            codes, plane = z_q[h]
+            for n, cols in enumerate(out_blocks):
+                bank = banks[(BANKS - 1 + len(out_blocks) * h + n) % BANKS]
                 nc.tensor.matmul_mx(
-                    out=y_sum[:], lhsT=w4_codes[:, cols].bitcast(FP8X4), lhsT_scale=w4_plane[:, cols],
-                    rhs=z_codes[:].bitcast(FP8X4), rhs_scale=z_plane[:], start=True, stop=True,
+                    out=bank[:], lhsT=w4_codes[:, cols].bitcast(FP8X4), lhsT_scale=w4_plane[:, cols],
+                    rhs=codes[:].bitcast(FP8X4), rhs_scale=plane[:], start=True, stop=True,
                 )
-                score = damp[h][n]
-                nc.vector.tensor_tensor(out=score, in0=y_sum[:], in1=score, op=ALU.mult)
-                nc.sync.dma_start(out=out[cols, halves[h]], in_=score)
+                piece = scores[:, h, n, :]
+                nc.vector.tensor_tensor(out=piece, in0=bank[:], in1=piece, op=ALU.mult)
+                nc.sync.dma_start(out=out[cols, epochs], in_=piece)

from contextlib import ExitStack

import concourse.mybir as mybir
from concourse.masks import make_identity

K, K2, H, N = 1536, 1024, 512, 384
TABLE, TABLE2 = 4096, 2048
EPOCHS, MARKED = 1024, 512
FLOPS = 2 * (K * H * EPOCHS + 2 * K2 * H * MARKED + 2 * H * N * EPOCHS)

F32 = mybir.dt.float32
BF16 = mybir.dt.bfloat16
I32 = mybir.dt.int32
U32 = mybir.dt.uint32
U16 = mybir.dt.uint16
U8 = mybir.dt.uint8
FP8X4 = mybir.dt.float8_e4m3fn_x4
FP4X4 = mybir.dt.float4_e2m1fn_x4
ALU = mybir.AluOpType
ACT = mybir.ActivationFunctionType

P = 128
SLOTS = 4
K_PASS = P * SLOTS
QUADS, QUAD = 4, 32
SCALE_ROWS = 4
GROUP = 16
HALF = 512
BANKS = 8
PASSES, PASSES2 = K // K_PASS, K2 // K_PASS
EARLY = SLOTS // 2


def tile_list_arousal_epoch_scorer_kernel(
    tc, tab_words, tab_scales, tab2_words, tab2_scales, w1, gain, w2, w3_words, w3_scales,
    wgs, w4, w5_words, w5_scales, offs, offs2, pos1, out,
):
    nc = tc.nc

    with ExitStack() as ctx:
        keep = ctx.enter_context(tc.tile_pool(name="keep", bufs=1))
        ring = ctx.enter_context(tc.tile_pool(name="ring", bufs=1))
        psum = ctx.enter_context(tc.psum_pool(name="psum", bufs=1))

        def held(shape, dtype, name):
            return keep.tile(shape, dtype, name=name, align_bytes=64)

        def in_buffer(buffer, shape, dtype, name):
            return ring.tile(shape, dtype, name=name, tag=buffer, bufs=1, align_bytes=64)

        def wide_f32(shape, name):
            return ring.tile(shape, F32, name=name, tag="wide_f32", bufs=4, align_bytes=64)

        def sine_row():
            return ring.tile([P, HALF], F32, name="sine", tag="sine", bufs=7, align_bytes=64)

        def wide_bf16(shape, name):
            return ring.tile(shape, BF16, name=name, tag="wide_bf16", bufs=4, align_bytes=64)

        banks = [psum.tile([P, HALF], F32, name="bank%d" % i) for i in range(BANKS)]

        def load_bytes(queue, tile, source):
            queue.dma_start(out=tile.bitcast(I32), in_=source.bitcast(I32))

        def load_plane_rows(tile, scales, quadrants):
            for q in quadrants:
                rows = scales[:, SCALE_ROWS * q : SCALE_ROWS * (q + 1), :]
                load_bytes(nc.sync, tile[QUAD * q : QUAD * q + SCALE_ROWS], rows.rearrange("g i c -> i g c"))

        def load_table(tile, words):
            load_bytes(nc.sync, tile[:], words.rearrange("p c t -> p (c t)"))

        def load_weight(tile, w, g):
            rows = w[K_PASS * g : K_PASS * (g + 1), :]
            nc.sync.dma_start(out=tile[:], in_=rows.rearrange("(p t) c -> p t c", t=SLOTS))
            return tile

        def round_dealt(copy, raw, buffer, name):
            rounded = in_buffer(buffer, [P, SLOTS * H], BF16, name)
            copy(
                out=rounded[:].rearrange("p (s m t) -> p m s t", s=SLOTS, t=SLOTS),
                in_=raw[:].rearrange("p t (m s) -> p m s t", s=SLOTS),
            )
            return rounded

        def interleave(rounded, rows):
            nc.vector.tensor_copy(
                out=rounded[:].rearrange("p (c t) -> p c t", t=SLOTS), in_=rows[:].rearrange("p t c -> p c t")
            )
            return rounded

        def quantize(rounded, name, codes_buffer=None, plane_buffer=None):
            width = rounded.shape[1] // SLOTS
            codes = in_buffer(codes_buffer or name + "_codes", [P, width], U32, name + "_codes")
            plane = in_buffer(plane_buffer or name + "_plane", [P, width], U8, name + "_plane")
            nc.vector.quantize_mx(out=codes[:].bitcast(FP8X4), scales=plane[:], in_=rounded[:])
            return codes, plane

        def gather(picked, window, offsets):
            nc.vector.tensor_copy(picked, window.indirect(offsets))

        blocks = [slice(P * i, P * (i + 1)) for i in range(SLOTS)]
        halves = [slice(HALF * h, HALF * (h + 1)) for h in range(EPOCHS // HALF)]

        offs_sb = keep.tile([P, EPOCHS // GROUP], U16, name="offs_sb")
        offs2_sb = keep.tile([P, MARKED // GROUP], U16, name="offs2_sb")
        pos_sb = keep.tile([P, MARKED // GROUP], U16, name="pos_sb")

        w3_given_planes = in_buffer("w3_given_planes", [P, PASSES2, H], U8, "w3_given_planes")
        tab2_planes = in_buffer("tab2_planes", [P, PASSES2, TABLE2], U8, "tab2_planes")
        tab_planes = in_buffer("tab_planes", [P, TABLE], U8, "tab_planes")
        w5_plane = held([P, 1, N], U8, "w5_plane")
        nc.gpsimd.memset(w3_given_planes[:].bitcast(I32), 0)
        nc.gpsimd.memset(tab2_planes[:, 0, :].bitcast(I32), 0)
        nc.vector.memset(tab2_planes[:, 1, :].bitcast(I32), 0)
        for tile in (tab_planes, w5_plane):
            nc.vector.memset(tile[:].bitcast(I32), 0)
        placed = [held([P, EPOCHS], F32, "placed%d" % t) for t in range(SLOTS)]
        for tile in placed:
            nc.vector.memset(tile[:], 0.0)

        tab2_sb = [in_buffer("tab2_%d" % g, [P, TABLE2], U32, "tab2_sb") for g in range(PASSES2)]
        tab_sb = [in_buffer("tab_%d" % g, [P, TABLE], U32, "tab_sb") for g in range(PASSES)]

        for q in range(QUADS):
            load_bytes(
                nc.gpsimd, tab_planes[QUAD * q : QUAD * q + SCALE_ROWS * PASSES, :],
                tab_scales[:, SCALE_ROWS * q : SCALE_ROWS * (q + 1), :],
            )
        nc.sync.dma_start(offs2_sb[:], offs2)
        nc.sync.dma_start(offs_sb[:], offs)
        nc.sync.dma_start(pos_sb[:], pos1)
        gain_sb = held([P, SLOTS], F32, "gain_sb")
        nc.sync.dma_start(out=gain_sb[:], in_=gain.rearrange("(p t) -> p t", t=SLOTS))
        load_table(tab2_sb[0], tab2_words[0])
        wgs_given = held([P, MARKED], F32, "wgs_given")
        nc.sync.dma_start(out=wgs_given[:], in_=wgs)
        w3_given = held([P, PASSES2, 2 * H], U8, "w3_given")
        load_bytes(nc.sync, w3_given[:], w3_words.rearrange("g p c -> p g c"))
        load_plane_rows(w3_given_planes, w3_scales, range(QUADS))
        load_table(tab2_sb[1], tab2_words[1])
        load_plane_rows(tab2_planes, tab2_scales, range(QUADS))
        w2_given = [
            load_weight(in_buffer("w2_first", [P, SLOTS, H], F32, "w2_given"), w2, 0),
            load_weight(wide_f32([P, SLOTS, H], "w2_given"), w2, 1),
        ]

        w3_sb = held([P, PASSES2, 2 * H], U8, "w3_sb")
        nc.scalar.copy(
            out=w3_sb[:].bitcast(U16).rearrange("p g (s m) -> p g s m", s=SLOTS),
            in_=w3_given[:].bitcast(U16).rearrange("p g (m s) -> p g s m", s=SLOTS),
        )

        identity = held([P, P], F32, "identity")
        make_identity(nc, identity[:])
        turn_bank = banks[2]
        for cols in blocks:
            nc.tensor.transpose(turn_bank[:, cols], wgs_given[:, cols], identity[:])
        wgs_turned = held([P, SLOTS, len(blocks), P], F32, "wgs_turned")
        by_slot = turn_bank[:].rearrange("j (b p t) -> j t b p", b=len(blocks), t=SLOTS)
        for t in range(SLOTS):
            nc.scalar.copy(
                out=wgs_turned[:, t].rearrange("j b (q p) -> j b q p", q=QUADS),
                in_=by_slot[:, t].unsqueeze(2).to_broadcast([P, len(blocks), QUADS, QUAD]),
            )
        wgs_sb = [held([P, MARKED], F32, "wgs_sb%d" % t) for t in range(SLOTS)]

        def turn_wgs_back(t, bank):
            for i, cols in enumerate(blocks):
                nc.tensor.transpose(bank[:, cols], wgs_turned[:, t, i, :], identity[:])
            nc.scalar.copy(out=wgs_sb[t][:], in_=bank[:])

        for t in range(EARLY):
            turn_wgs_back(t, banks[BANKS - EARLY + t])

        v2 = [held([P, MARKED], U32, "v2_first")]
        gather(v2[0][:], tab2_sb[0][:], offs2_sb[:])
        w3_planes = in_buffer("tab2_0", [P, PASSES2, H], U8, "w3_planes")
        nc.vector.tensor_copy(
            out=w3_planes[:].rearrange("p g (s m) -> p g s m", s=SLOTS),
            in_=w3_given_planes[:].rearrange("p g (m s) -> p g s m", s=SLOTS),
        )
        v2_planes = [held([P, MARKED], U8, "v2_plane%d" % g) for g in range(PASSES2)]
        for g in range(PASSES2):
            gather(v2_planes[g][:], tab2_planes[:, g, :], offs2_sb[:])
        v2.append(in_buffer("tab2_planes", [P, MARKED], U32, "v2_last"))
        gather(v2[1][:], tab2_sb[1][:], offs2_sb[:])
        w2_rounded = [
            round_dealt(nc.scalar.copy, w2_given[0], "rounded", "w2_rounded"),
            round_dealt(nc.vector.tensor_copy, w2_given[1], "tab2_1", "w2_rounded"),
        ]
        w2_q = [quantize(w2_rounded[0], "w2_0", plane_buffer="w3_given_planes"), quantize(w2_rounded[1], "w2_1")]

        w1_given = []
        for g in range(PASSES):
            w1_given.append(load_weight(wide_f32([P, SLOTS, H], "w1_given"), w1, g))
            load_table(tab_sb[g], tab_words[g])
        w4_given = load_weight(wide_f32([P, SLOTS, N], "w4_given"), w4, 0)
        w5_sb = held([P, N], U32, "w5_sb")
        load_table(w5_sb, w5_words[0])
        load_plane_rows(w5_plane, w5_scales, range(QUADS))

        def magnitude_pass(g, t, bank):
            nc.tensor.matmul_mx(
                out=bank[:], lhsT=w3_sb[:, g, 2 * P * t : 2 * P * (t + 1)].bitcast(FP4X4),
                lhsT_scale=w3_planes[:, g, blocks[t]], rhs=v2[g][:].bitcast(FP8X4), rhs_scale=v2_planes[g][:],
                start=(g == 0), stop=(g == PASSES2 - 1),
            )

        def signed_pass(g, t, bank):
            codes, plane = w2_q[g]
            nc.tensor.matmul_mx(
                out=bank[:], lhsT=codes[:, blocks[t]].bitcast(FP8X4), lhsT_scale=plane[:, blocks[t]],
                rhs=v2[g][:].bitcast(FP8X4), rhs_scale=v2_planes[g][:],
                start=(g == 0), stop=(g == PASSES2 - 1),
            )

        magnitudes = in_buffer("w2_first", [P, SLOTS, MARKED], F32, "magnitudes")

        def place(t, signed_bank):
            b_rows = in_buffer("b_%d" % t, [P, MARKED], F32, "b_rows")
            nc.vector.tensor_tensor(out=b_rows[:], in0=signed_bank[:], in1=magnitudes[:, t, :], op=ALU.mult)
            nc.vector.tensor_tensor(placed[t][:].indirect(pos_sb[:]), b_rows[:], wgs_sb[t][:], ALU.mult)

        for t in range(SLOTS):
            for g in range(PASSES2):
                magnitude_pass(g, t, banks[t % 2])
                if t < EARLY:
                    signed_pass(g, t, banks[SLOTS + t])
            nc.scalar.activation(out=magnitudes[:, t, :], in_=banks[t % 2][:], func=ACT.Abs)
            if t < EARLY:
                place(t, banks[SLOTS + t])
        for t in range(EARLY, SLOTS):
            turn_wgs_back(t, banks[t % 2])

        rounded_buffers = ("tab2_1", "rounded", "tab2_1")
        codes_buffers = ("b_0", None, None)
        picked_buffers = ("b_1", "tab_planes", "v_last")
        w1_q, v = [], []
        for g in range(PASSES):
            rounded = round_dealt(nc.scalar.copy, w1_given[g], rounded_buffers[g], "w1_rounded")
            w1_q.append(quantize(rounded, "w1_%d" % g, codes_buffer=codes_buffers[g]))
            v.append(in_buffer(picked_buffers[g], [P, EPOCHS], U32, "v"))
            if g < PASSES - 1:
                gather(v[g][:], tab_sb[g][:], offs_sb[:])
            else:
                for epochs in halves:
                    gather(v[g][:, epochs], tab_sb[g][:], offs_sb[:, epochs.start // GROUP : epochs.stop // GROUP])
            if g == 0:
                v_planes = in_buffer("tab_0", [P, EPOCHS], U8, "v_planes")
                gather(v_planes[:], tab_planes[:], offs_sb[:])

        phase = [[banks[SLOTS * h + t] for t in range(SLOTS)] for h in range(len(halves))]
        for h, epochs in enumerate(halves):
            for g in range(PASSES):
                codes, plane = w1_q[g]
                for t in range(SLOTS):
                    nc.tensor.matmul_mx(
                        out=phase[h][t][:], lhsT=codes[:, blocks[t]].bitcast(FP8X4), lhsT_scale=plane[:, blocks[t]],
                        rhs=v[g][:, epochs].bitcast(FP8X4), rhs_scale=v_planes[SCALE_ROWS * g :, epochs],
                        start=(g == 0), stop=(g == PASSES - 1),
                    )

        minus_two_gain = held([P, SLOTS], F32, "minus_two_gain")
        nc.vector.tensor_scalar(out=minus_two_gain[:], in0=gain_sb[:], scalar1=-2.0, scalar2=None, op0=ALU.mult)

        def apply_gain(rows, squares, t):
            nc.scalar.activation(
                out=rows[:, t, :], in_=squares[t][:], func=ACT.Identity,
                scale=minus_two_gain[:, t : t + 1], bias=gain_sb[:, t : t + 1],
            )

        a_rows, a_q = [], []
        for h in range(len(halves)):
            rows = wide_f32([P, SLOTS, HALF], "a_rows")
            sines = [sine_row() for t in range(SLOTS)]
            for step in range(SLOTS + 1):
                if step < SLOTS:
                    nc.scalar.activation(out=sines[step][:], in_=phase[h][step][:], func=ACT.Sin, scale=0.5)
                if h == 0 and step == 0:
                    w4_rounded = in_buffer("tab_2", [P, SLOTS * N], BF16, "w4_rounded")
                    w4_codes, w4_plane = quantize(interleave(w4_rounded, w4_given), "w4")
                if h == 0 and step < SLOTS - EARLY:
                    for g in range(PASSES2):
                        signed_pass(g, EARLY + step, phase[h][step])
                    place(EARLY + step, phase[h][step])
                if step > 0:
                    nc.scalar.activation(out=sines[step - 1][:], in_=sines[step - 1][:], func=ACT.Square)
                if step > 1:
                    apply_gain(rows, sines, step - 2)
            apply_gain(rows, sines, SLOTS - 1)
            a_rows.append(rows)
            a_q.append(quantize(interleave(wide_bf16([P, SLOTS * HALF], "a_rounded"), rows), "a_%d" % h))

        out_blocks = blocks[: N // P]
        scores = in_buffer("tab_0", [P, len(halves), len(out_blocks), HALF], F32, "scores")

        def damp(h):
            codes, plane = a_q[h]
            pieces = [scores[:, h, n, :] for n in range(len(out_blocks))]
            for n, cols in enumerate(out_blocks):
                bank = banks[1 + len(out_blocks) * h + n]
                nc.tensor.matmul_mx(
                    out=bank[:], lhsT=w5_sb[:, cols].bitcast(FP8X4), lhsT_scale=w5_plane[:, 0, cols],
                    rhs=codes[:].bitcast(FP8X4), rhs_scale=plane[:], start=True, stop=True,
                )
                nc.scalar.activation(out=pieces[n], in_=bank[:], func=ACT.Abs)
            for piece in pieces:
                nc.scalar.activation(out=piece, in_=piece, func=ACT.Abs_reciprocal_sqrt, bias=1.0)
            for piece in pieces:
                nc.scalar.activation(out=piece, in_=piece, func=ACT.Square)

        def quantize_z(h):
            z_rows = wide_bf16([P, SLOTS, HALF], "z_rows")
            for t in range(SLOTS):
                nc.vector.tensor_tensor(
                    out=z_rows[:, t, :], in0=a_rows[h][:, t, :], in1=placed[t][:, halves[h]], op=ALU.add
                )
            return quantize(interleave(wide_bf16([P, SLOTS * HALF], "z_rounded"), z_rows), "z_%d" % h)

        z_q = []
        for h in range(len(halves)):
            damp(h)
            z_q.append(quantize_z(h))

        for h, epochs in enumerate(halves):
            codes, plane = z_q[h]
            for n, cols in enumerate(out_blocks):
                bank = banks[(BANKS - 1 + len(out_blocks) * h + n) % BANKS]
                nc.tensor.matmul_mx(
                    out=bank[:], lhsT=w4_codes[:, cols].bitcast(FP8X4), lhsT_scale=w4_plane[:, cols],
                    rhs=codes[:].bitcast(FP8X4), rhs_scale=plane[:], start=True, stop=True,
                )
                piece = scores[:, h, n, :]
                nc.vector.tensor_tensor(out=piece, in0=bank[:], in1=piece, op=ALU.mult)
                nc.sync.dma_start(out=out[cols, epochs], in_=piece)
